import numpy as np
import ml_dtypes


def mxq(x, axis, fmt="e4m3"):
    dtype, down = {"e4m3": (ml_dtypes.float8_e4m3fn, 7), "e5m2": (ml_dtypes.float8_e5m2, 14)}[fmt]
    v = np.moveaxis(np.asarray(x, np.float32).astype(ml_dtypes.bfloat16).astype(np.float64), axis, -1)
    blocks = v.reshape(v.shape[:-1] + (-1, 32))
    amax = np.abs(blocks).max(-1, keepdims=True)
    byte = np.maximum(np.where(amax > 0, np.frexp(amax)[1] - 1 + 127, 0) - down, 1)
    scale = np.exp2(byte - 127.0)
    codes = (blocks / scale).astype(np.float32).astype(dtype).astype(np.float64)
    return np.moveaxis((codes * scale).reshape(v.shape), -1, axis)


WIDE = False


def mx_kscale(k):
    if not WIDE:
        return np.ones(k)
    levels = np.array([18, -18])
    if k % 512:
        return np.exp2(np.random.permutation(np.resize(levels, k // 32))).repeat(32)
    a = np.empty((k // 512, 16))
    for p in range(k // 512):
        a[p, :8] = np.random.permutation(np.resize(levels, 8))
        for g in range(8):
            far = levels[np.abs(levels - a[p, g]) >= 10]
            a[p, g + 8] = far[np.random.randint(len(far))]
    return np.exp2(a.ravel()).repeat(32)


def f64(x):
    return np.asarray(x).astype(np.float64)


def striped(idx):
    return np.tile(np.asarray(idx).reshape(-1, 16).T, (8, 1)).astype(np.uint16)


def unstriped(offs):
    return offs[:16].T.reshape(-1).astype(np.int64)


def setup_inputs():
    n = np.random.standard_normal
    uni = np.random.uniform
    idx = np.random.permutation(2048)[:512]
    f_d = mx_kscale(512)
    return {
        "xT": (n((512, 512)) * f_d[:, None]).astype(np.float32),
        "wa": (n((512, 2048)) / np.sqrt(512) / f_d[:, None]).astype(np.float32),
        "wb": (n((512, 2048)) / np.sqrt(512) / f_d[:, None]).astype(np.float32),
        "us": (uni(0.75, 1.3, (512, 1))).astype(np.float32),
        "ts": np.tile(uni(0.75, 1.3, 2048), (128, 1)).astype(np.float32),
        "xx": (uni(0.75, 1.3, (512, 1))).astype(np.float32),
        "y": (n((512, 512))).astype(np.float32),
        "offs": striped(idx),
    }


def reference(xT, wa, wb, us, ts, xx, y, offs):
    idx = unstriped(offs)
    wa_i = f64(wa)[:, idx]
    wb_i = f64(wb)[:, idx]
    ts_i = f64(ts)[:1][:, idx]
    q_xT = mxq(f64(xT), 0, "e4m3")
    sa = q_xT.T @ mxq(wa_i, 0, "e4m3")
    za = f64(us) * ts_i * sa
    ga = za - f64(y)
    sb = q_xT.T @ mxq(wb_i, 0, "e4m3")
    zb = f64(us) * ts_i * sb
    gb = zb - f64(y)
    ip = (ga * gb).sum(-1, keepdims=True)
    res = f64(xx) * ip
    out = res.T
    return out

@@ -1,0 +1,188 @@
+from contextlib import ExitStack
+
+import concourse.mybir as mybir
+from concourse.masks import make_identity
+
+D, R, SLOTS, T = 512, 512, 512, 2048
+P = 128
+PACK = 4
+TILES = R // P
+HALF = 256
+
+F32 = mybir.dt.float32
+BF16 = mybir.dt.bfloat16
+U32 = mybir.dt.uint32
+U16 = mybir.dt.uint16
+U8 = mybir.dt.uint8
+FP8X4 = mybir.dt.float8_e4m3fn_x4
+MULT = mybir.AluOpType.mult
+SUB = mybir.AluOpType.subtract
+COPY = mybir.ActivationFunctionType.Copy
+
+FLOPS = 2 * 2 * D * R * SLOTS
+BYTES = 4 * (D * R + 2 * D * T + 2 * R + T + R * SLOTS + R) + 2 * P * SLOTS // 16
+
+
+def tile_attend_gtrace_sq_kernel(tc, xT, wa, wb, us, ts, xx, y, offs, out):
+    nc = tc.nc
+    with ExitStack() as ctx:
+        keep = ctx.enter_context(tc.tile_pool(name="keep", bufs=1))
+        psum = ctx.enter_context(tc.psum_pool(name="psum", bufs=1))
+
+        offsets = keep.tile([P, SLOTS // 16], U16, name="offsets")
+        wa_planes = [keep.tile([P, T], F32, name="wa%d" % t) for t in range(PACK)]
+        wb_planes = [keep.tile([P, T], F32, name="wb%d" % t) for t in range(PACK)]
+        x_raw = [keep.tile([P, PACK, HALF], F32, name="x_raw%d" % u) for u in range(2)]
+        y_sb = [keep.tile([P, 2, SLOTS], F32, name="y_sb%d" % u) for u in range(2)]
+        wa_v = wa.rearrange("(p t) w -> p t w", t=PACK)
+        wb_v = wb.rearrange("(p t) w -> p t w", t=PACK)
+        x_v = xT.rearrange("(p t) r -> p t r", t=PACK)
+        y_v = y.rearrange("(c p) i -> p c i", p=P)
+
+        nc.sync.dma_start(out=wa_planes[0][:], in_=wa_v[:, 0, :])
+        nc.sync.dma_start(offsets[:], offs)
+        ts_stage = keep.tile([1, T], F32, name="ts_stage")
+        us_stage = keep.tile([2 * TILES, P], F32, name="us_stage")
+        nc.scalar.dma_start(out=ts_stage[:], in_=ts[0:1, :])
+        nc.scalar.dma_start(out=us_stage[0:TILES, :], in_=us.rearrange("(c p) o -> c (p o)", p=P))
+        nc.scalar.dma_start(out=us_stage[TILES:2 * TILES, :], in_=xx.rearrange("(c p) o -> c (p o)", p=P))
+        for t in range(1, PACK):
+            nc.sync.dma_start(out=wa_planes[t][:], in_=wa_v[:, t, :])
+        for u in range(2):
+            nc.sync.dma_start(out=x_raw[u][:], in_=x_v[:, :, u * HALF:(u + 1) * HALF])
+        for u in range(2):
+            nc.sync.dma_start(out=y_sb[u][:], in_=y_v[:, 2 * u:2 * u + 2, :])
+        for t in range(PACK):
+            nc.sync.dma_start(out=wb_planes[t][:], in_=wb_v[:, t, :])
+
+        ts_win = keep.tile([P, T], F32, name="ts_win")
+        row_scales = keep.tile([P, P], F32, name="row_scales")
+        res_cols = keep.tile([P, P], F32, name="res_cols", align_bytes=64)
+        ident = keep.tile([P, P], F32, name="ident")
+        nc.vector.memset(row_scales[:], 0.0)
+        nc.vector.memset(ts_win[:], 0.0)
+        nc.vector.memset(res_cols[:], 0.0)
+        make_identity(nc, ident[:])
+        nc.scalar.activation(ts_win[0:1, :], ts_stage[:], COPY)
+        nc.scalar.copy(out=row_scales[0:2 * TILES, :], in_=us_stage[:])
+
+        bank = psum.tile([P, SLOTS], F32, name="bank6")
+        nc.tensor.transpose(bank[:, 0:P], row_scales[:], ident[:])
+        usxx = keep.tile([P, 2 * TILES], F32, name="usxx")
+        nc.scalar.copy(out=usxx[:], in_=bank[:, 0:2 * TILES])
+        us_xx = keep.tile([P, TILES], F32, name="us_xx")
+        nc.vector.tensor_tensor(us_xx[:], usxx[:, 0:TILES], usxx[:, TILES:2 * TILES], MULT)
+
+        ts_row = keep.tile([P, SLOTS], F32, name="ts_row")
+        nc.vector.tensor_copy(ts_row[:], ts_win[:].indirect(offsets[:]))
+        bank = psum.tile([P, TILES, P], F32, name="bank4")
+        for b in range(4):
+            nc.tensor.transpose(bank[:, b, :], ts_row[:, b * P:(b + 1) * P], ident[:])
+        ts_cols = keep.tile([P, 4], F32, name="ts_cols")
+        nc.scalar.copy(out=ts_cols[:], in_=bank[:, :, 0])
+        bank = psum.tile([P, 4, P], F32, name="bank5")
+        for b in range(4):
+            nc.tensor.transpose(bank[:, b, :], ts_cols[:, b:b + 1].to_broadcast([P, P]), ident[:])
+        ts_all = keep.tile([P, SLOTS], F32, name="ts_all")
+        nc.scalar.copy(out=ts_all[:], in_=bank[:].rearrange("p b m -> p (b m)"))
+
+        def operand(name):
+            grouped = keep.tile([P, SLOTS, PACK], BF16, name=name + "_grouped", align_bytes=64)
+            codes = keep.tile([P, SLOTS], U32, name=name + "_codes", align_bytes=64)
+            scales = keep.tile([P, SLOTS], U8, name=name + "_scales", align_bytes=64)
+            return grouped, codes, scales
+
+        def quantize(op, c0, c1):
+            grouped, codes, scales = op
+            nc.vector.quantize_mx(
+                out=codes[:, c0:c1].bitcast(FP8X4),
+                scales=scales[:, c0:c1],
+                in_=grouped[:, c0:c1, :].rearrange("p w t -> p (w t)"),
+            )
+
+        def gather(op, planes, t, c0, c1):
+            nc.vector.tensor_copy(op[0][:, c0:c1, t], planes[t][:].indirect(offsets[:, c0 // 16:c1 // 16]))
+
+        def scores(dst, w_op, c, c0, c1):
+            rows = slice(c * P, (c + 1) * P)
+            nc.tensor.matmul_mx(
+                out=dst[:, c0:c1],
+                lhsT=x_op[1][:, rows].bitcast(FP8X4),
+                lhsT_scale=x_op[2][:, rows],
+                rhs=w_op[1][:, c0:c1].bitcast(FP8X4),
+                rhs_scale=w_op[2][:, c0:c1],
+                start=True,
+                stop=True,
+            )
+
+        x_op = operand("x")
+        a_op = operand("a")
+        b_op = operand("b")
+
+        for t in range(PACK):
+            gather(a_op, wa_planes, t, 0, SLOTS)
+        for u in range(2):
+            nc.scalar.copy(
+                out=x_op[0][:, u * HALF:(u + 1) * HALF, :].rearrange("p (c i) t -> p c t i", i=4),
+                in_=x_raw[u][:].rearrange("p t (c i) -> p c t i", i=4),
+            )
+        quantize(a_op, 0, SLOTS)
+        quantize(x_op, 0, HALF)
+
+        sa = [psum.tile([P, SLOTS], F32, name="bank%d" % c) for c in range(TILES)]
+        za = [keep.tile([P, SLOTS], F32, name="za%d" % c) for c in range(TILES)]
+        ga = [keep.tile([P, SLOTS], F32, name="ga%d" % c) for c in range(TILES)]
+        h = [keep.tile([P, SLOTS], F32, name="h%d" % c) for c in range(TILES)]
+        spare = keep.tile([P, SLOTS], F32, name="spare")
+        e = keep.tile([P, TILES], F32, name="e")
+        acc = keep.tile([P, TILES], F32, name="acc")
+
+        def op1(c):
+            nc.vector.scalar_tensor_tensor(za[c][:], sa[c][:], usxx[:, c:c + 1], ts_all[:], MULT, MULT)
+
+        def op2(c):
+            nc.vector.tensor_tensor(ga[c][:], za[c][:], y_sb[c // 2][:, c % 2, :], SUB)
+
+        def op3(c):
+            nc.vector.tensor_tensor(h[c][:], ga[c][:], ts_all[:], MULT)
+
+        def op4(c):
+            nc.vector.scalar_tensor_tensor(spare[:], ga[c][:], usxx[:, TILES + c:TILES + c + 1], y_sb[c // 2][:, c % 2, :],
+                                           MULT, MULT, accum_out=e[:, c:c + 1])
+
+        for u in range(2):
+            c0, c1 = 2 * u, 2 * u + 1
+            scores(sa[c0], a_op, c0, 0, SLOTS)
+            scores(sa[c1], a_op, c1, 0, SLOTS)
+            if u == 0:
+                quantize(x_op, HALF, R)
+            op1(c0)
+            op1(c1)
+            op2(c0)
+            op2(c1)
+            op3(c0)
+            op3(c1)
+            op4(c0)
+            op4(c1)
+            gather(b_op, wb_planes, u, 0, SLOTS)
+        gather(b_op, wb_planes, 2, 0, SLOTS)
+        gather(b_op, wb_planes, 3, 0, HALF)
+        gather(b_op, wb_planes, 3, HALF, SLOTS)
+        quantize(b_op, 0, HALF)
+        quantize(b_op, HALF, SLOTS)
+
+        sb = [psum.tile([P, SLOTS], F32, name="bank%d" % (TILES + c)) for c in range(TILES)]
+        scores(sb[0], b_op, 0, 0, HALF)
+        scores(sb[0], b_op, 0, HALF, SLOTS)
+        for c in range(1, TILES):
+            scores(sb[c], b_op, c, 0, SLOTS)
+        for c in range(TILES):
+            nc.vector.scalar_tensor_tensor(spare[:], sb[c][:], us_xx[:, c:c + 1], h[c][:], MULT, MULT,
+                                           accum_out=acc[:, c:c + 1])
+        nc.vector.tensor_tensor(res_cols[:, 0:P:32], acc[:], e[:], SUB)
+        res_rows = keep.tile([P, P], F32, name="res_rows", align_bytes=64)
+        nc.vector.transpose(res_rows[:], res_cols[:])
+        nc.sync.dma_start(
+            out=out.rearrange("o (c q j) -> q (o c) j", q=4, j=32),
+            in_=res_rows[0:P:32, :].rearrange("q (c j) -> q c j", j=32),
+        )

@@ -39,14 +39,13 @@ def tile_attend_gtrace_sq_kernel(tc, xT, wa, wb, us, ts, xx, y, offs, out):
         x_v = xT.rearrange("(p t) r -> p t r", t=PACK)
         y_v = y.rearrange("(c p) i -> p c i", p=P)
 
-        nc.sync.dma_start(out=wa_planes[0][:], in_=wa_v[:, 0, :])
-        nc.sync.dma_start(offsets[:], offs)
         ts_stage = keep.tile([1, T], F32, name="ts_stage")
+        nc.sync.dma_start(out=ts_stage[:], in_=ts[0:1, :])
+        nc.sync.dma_start(offsets[:], offs)
         us_stage = keep.tile([2 * TILES, P], F32, name="us_stage")
-        nc.scalar.dma_start(out=ts_stage[:], in_=ts[0:1, :])
         nc.scalar.dma_start(out=us_stage[0:TILES, :], in_=us.rearrange("(c p) o -> c (p o)", p=P))
         nc.scalar.dma_start(out=us_stage[TILES:2 * TILES, :], in_=xx.rearrange("(c p) o -> c (p o)", p=P))
-        for t in range(1, PACK):
+        for t in range(PACK):
             nc.sync.dma_start(out=wa_planes[t][:], in_=wa_v[:, t, :])
         for u in range(2):
             nc.sync.dma_start(out=x_raw[u][:], in_=x_v[:, :, u * HALF:(u + 1) * HALF])
@@ -63,10 +62,10 @@ def tile_attend_gtrace_sq_kernel(tc, xT, wa, wb, us, ts, xx, y, offs, out):
         nc.vector.memset(ts_win[:], 0.0)
         nc.vector.memset(res_cols[:], 0.0)
         make_identity(nc, ident[:])
-        nc.scalar.activation(ts_win[0:1, :], ts_stage[:], COPY)
-        nc.scalar.copy(out=row_scales[0:2 * TILES, :], in_=us_stage[:])
+        nc.vector.tensor_copy(ts_win[0:1, :], ts_stage[:])
+        nc.scalar.activation(row_scales[0:2 * TILES, :], us_stage[:], COPY)
 
-        bank = psum.tile([P, SLOTS], F32, name="bank6")
+        bank = psum.tile([P, SLOTS], F32, name="bank5")
         nc.tensor.transpose(bank[:, 0:P], row_scales[:], ident[:])
         usxx = keep.tile([P, 2 * TILES], F32, name="usxx")
         nc.scalar.copy(out=usxx[:], in_=bank[:, 0:2 * TILES])
@@ -75,12 +74,12 @@ def tile_attend_gtrace_sq_kernel(tc, xT, wa, wb, us, ts, xx, y, offs, out):
 
         ts_row = keep.tile([P, SLOTS], F32, name="ts_row")
         nc.vector.tensor_copy(ts_row[:], ts_win[:].indirect(offsets[:]))
-        bank = psum.tile([P, TILES, P], F32, name="bank4")
+        bank = psum.tile([P, TILES, P], F32, name="bank6")
         for b in range(4):
             nc.tensor.transpose(bank[:, b, :], ts_row[:, b * P:(b + 1) * P], ident[:])
         ts_cols = keep.tile([P, 4], F32, name="ts_cols")
         nc.scalar.copy(out=ts_cols[:], in_=bank[:, :, 0])
-        bank = psum.tile([P, 4, P], F32, name="bank5")
+        bank = psum.tile([P, 4, P], F32, name="bank7")
         for b in range(4):
             nc.tensor.transpose(bank[:, b, :], ts_cols[:, b:b + 1].to_broadcast([P, P]), ident[:])
         ts_all = keep.tile([P, SLOTS], F32, name="ts_all")
@@ -119,59 +118,111 @@ def tile_attend_gtrace_sq_kernel(tc, xT, wa, wb, us, ts, xx, y, offs, out):
         a_op = operand("a")
         b_op = operand("b")
 
-        for t in range(PACK):
-            gather(a_op, wa_planes, t, 0, SLOTS)
-        for u in range(2):
-            nc.scalar.copy(
-                out=x_op[0][:, u * HALF:(u + 1) * HALF, :].rearrange("p (c i) t -> p c t i", i=4),
-                in_=x_raw[u][:].rearrange("p t (c i) -> p c t i", i=4),
-            )
-        quantize(a_op, 0, SLOTS)
-        quantize(x_op, 0, HALF)
+        def interleave(copy, grouped, planes):
+            copy(out=grouped.rearrange("p (c i) t -> p c t i", i=4), in_=planes.rearrange("p t (c i) -> p c t i", i=4))
 
-        sa = [psum.tile([P, SLOTS], F32, name="bank%d" % c) for c in range(TILES)]
-        za = [keep.tile([P, SLOTS], F32, name="za%d" % c) for c in range(TILES)]
+        def interleave_x(copy, c):
+            interleave(copy, x_op[0][:, c * P:(c + 1) * P, :], x_raw[c // 2][:, :, (c % 2) * P:(c % 2 + 1) * P])
+
+        a_pair = keep.tile([P, 2, SLOTS], BF16, name="a_pair")
+        for t in range(2):
+            nc.vector.tensor_copy(a_pair[:, t, :], wa_planes[t][:].indirect(offsets[:]))
+        nc.scalar.copy(out=a_op[0][:, :, 0:2], in_=a_pair[:].rearrange("p t s -> p s t"))
+        gather(a_op, wa_planes, 2, 0, SLOTS)
+        gather(a_op, wa_planes, 3, 0, HALF)
+        gather(a_op, wa_planes, 3, HALF, SLOTS)
+        for c in range(3):
+            interleave_x(nc.scalar.copy, c)
+        quantize(a_op, 0, HALF)
+        quantize(a_op, HALF, SLOTS)
+        quantize(x_op, 0, P)
+        quantize(x_op, P, HALF)
+        interleave_x(nc.vector.tensor_copy, 3)
+        quantize(x_op, HALF, R)
+
+        za = [keep.tile([P, SLOTS], F32, name="za%d" % c) for c in range(2)]
         ga = [keep.tile([P, SLOTS], F32, name="ga%d" % c) for c in range(TILES)]
         h = [keep.tile([P, SLOTS], F32, name="h%d" % c) for c in range(TILES)]
         spare = keep.tile([P, SLOTS], F32, name="spare")
         e = keep.tile([P, TILES], F32, name="e")
         acc = keep.tile([P, TILES], F32, name="acc")
+        b_planes = keep.tile([P, 4, PACK, P], BF16, name="b_planes")
 
-        def op1(c):
-            nc.vector.scalar_tensor_tensor(za[c][:], sa[c][:], usxx[:, c:c + 1], ts_all[:], MULT, MULT)
+        def y_of(c):
+            return y_sb[c // 2][:, c % 2, :]
 
-        def op2(c):
-            nc.vector.tensor_tensor(ga[c][:], za[c][:], y_sb[c // 2][:, c % 2, :], SUB)
-
-        def op3(c):
-            nc.vector.tensor_tensor(h[c][:], ga[c][:], ts_all[:], MULT)
-
-        def op4(c):
-            nc.vector.scalar_tensor_tensor(spare[:], ga[c][:], usxx[:, TILES + c:TILES + c + 1], y_sb[c // 2][:, c % 2, :],
+        def with_targets(c):
+            nc.vector.scalar_tensor_tensor(spare[:], ga[c][:], usxx[:, TILES + c:TILES + c + 1], y_of(c),
                                            MULT, MULT, accum_out=e[:, c:c + 1])
 
-        for u in range(2):
-            c0, c1 = 2 * u, 2 * u + 1
-            scores(sa[c0], a_op, c0, 0, SLOTS)
-            scores(sa[c1], a_op, c1, 0, SLOTS)
-            if u == 0:
-                quantize(x_op, HALF, R)
-            op1(c0)
-            op1(c1)
-            op2(c0)
-            op2(c1)
-            op3(c0)
-            op3(c1)
-            op4(c0)
-            op4(c1)
-            gather(b_op, wb_planes, u, 0, SLOTS)
-        gather(b_op, wb_planes, 2, 0, SLOTS)
-        gather(b_op, wb_planes, 3, 0, HALF)
-        gather(b_op, wb_planes, 3, HALF, SLOTS)
+        def scale_slots(banks, name):
+            scaled = keep.tile([P, 4, HALF], F32, name=name)
+            for b in range(4):
+                nc.scalar.activation(scaled[:, b, :], banks[b // 2][:, b % 2, :], COPY, scale=ts_cols[:, b:b + 1])
+            return scaled
+
+        def turn_back(scaled, j, name):
+            bank = psum.tile([P, SLOTS], F32, name=name)
+            for b in range(4):
+                nc.tensor.transpose(bank[:, b * P:(b + 1) * P], scaled[:, b, j * P:(j + 1) * P], ident[:])
+            return bank
+
+        def weigh_turned(u, names):
+            banks = [psum.tile([P, 2, HALF], F32, name=n) for n in names]
+            for b in range(4):
+                for j in range(2):
+                    nc.tensor.transpose(banks[b // 2][:, b % 2, j * P:(j + 1) * P], ga[2 * u + j][:, b * P:(b + 1) * P], ident[:])
+            return scale_slots(banks, "hT%d" % u)
+
+        def weigh_back(u, scaled, names):
+            for j in range(2):
+                bank = turn_back(scaled, j, names[j])
+                nc.scalar.copy(out=h[2 * u + j][:], in_=bank[:])
+
+        def gather_b(t):
+            nc.vector.tensor_copy(b_planes[:, :, t, :], wb_planes[t][:].indirect(offsets[:]))
+
+        sa = [psum.tile([P, SLOTS], F32, name="bank%d" % c) for c in range(2)]
+        scores(sa[0], a_op, 0, 0, SLOTS)
+        scores(sa[1], a_op, 1, 0, SLOTS)
+        nc.vector.scalar_tensor_tensor(za[0][:], sa[0][:], usxx[:, 0:1], ts_all[:], MULT, MULT)
+        saT = [psum.tile([P, 2, HALF], F32, name="bank%d" % (2 + j)) for j in range(2)]
+        for b in range(4):
+            nc.tensor.matmul_mx(
+                out=saT[b // 2][:, b % 2, :],
+                lhsT=a_op[1][:, b * P:(b + 1) * P].bitcast(FP8X4),
+                lhsT_scale=a_op[2][:, b * P:(b + 1) * P],
+                rhs=x_op[1][:, HALF:R].bitcast(FP8X4),
+                rhs_scale=x_op[2][:, HALF:R],
+                start=True,
+                stop=True,
+            )
+        uT = scale_slots(saT, "uT")
+        u_banks = [turn_back(uT, j, "bank%d" % (4 + j)) for j in range(2)]
+        nc.vector.scalar_tensor_tensor(za[1][:], sa[1][:], usxx[:, 1:2], ts_all[:], MULT, MULT)
+        for c in range(2):
+            nc.vector.tensor_tensor(ga[c][:], za[c][:], y_of(c), SUB)
+        hT0 = weigh_turned(0, ("bank6", "bank7"))
+        with_targets(0)
+        gather_b(0)
+        for j in range(2):
+            nc.vector.scalar_tensor_tensor(ga[2 + j][:], u_banks[j][:], usxx[:, 2 + j:3 + j], y_of(2 + j), MULT, SUB)
+        hT1 = weigh_turned(1, ("bank2", "bank3"))
+        weigh_back(0, hT0, ("bank0", "bank1"))
+        weigh_back(1, hT1, ("bank4", "bank5"))
+        with_targets(1)
+        gather_b(1)
+        with_targets(2)
+        gather_b(2)
+        for b in range(4):
+            nc.vector.tensor_copy(b_planes[:, b, 3, :], wb_planes[3][:].indirect(offsets[:, b * 8:(b + 1) * 8]))
+        for b in range(4):
+            interleave(nc.scalar.copy if b < 2 else nc.vector.tensor_copy, b_op[0][:, b * P:(b + 1) * P, :], b_planes[:, b, :, :])
         quantize(b_op, 0, HALF)
         quantize(b_op, HALF, SLOTS)
+        with_targets(3)
 
-        sb = [psum.tile([P, SLOTS], F32, name="bank%d" % (TILES + c)) for c in range(TILES)]
+        sb = [psum.tile([P, SLOTS], F32, name="bank%d" % n) for n in (6, 7, 0, 1)]
         scores(sb[0], b_op, 0, 0, HALF)
         scores(sb[0], b_op, 0, HALF, SLOTS)
         for c in range(1, TILES):

@@ -143,7 +143,7 @@ def tile_attend_gtrace_sq_kernel(tc, xT, wa, wb, us, ts, xx, y, offs, out):
         za = [keep.tile([P, SLOTS], F32, name="za%d" % c) for c in range(2)]
         ga = [keep.tile([P, SLOTS], F32, name="ga%d" % c) for c in range(TILES)]
         h = [keep.tile([P, SLOTS], F32, name="h%d" % c) for c in range(TILES)]
-        spare = keep.tile([P, SLOTS], F32, name="spare")
+        spare = [keep.tile([P, SLOTS], F32, name="spare%d" % n) for n in range(2 * TILES)]
         e = keep.tile([P, TILES], F32, name="e")
         acc = keep.tile([P, TILES], F32, name="acc")
         b_planes = keep.tile([P, 4, PACK, P], BF16, name="b_planes")
@@ -152,7 +152,7 @@ def tile_attend_gtrace_sq_kernel(tc, xT, wa, wb, us, ts, xx, y, offs, out):
             return y_sb[c // 2][:, c % 2, :]
 
         def with_targets(c):
-            nc.vector.scalar_tensor_tensor(spare[:], ga[c][:], usxx[:, TILES + c:TILES + c + 1], y_of(c),
+            nc.vector.scalar_tensor_tensor(spare[c][:], ga[c][:], usxx[:, TILES + c:TILES + c + 1], y_of(c),
                                            MULT, MULT, accum_out=e[:, c:c + 1])
 
         def scale_slots(banks, name):
@@ -228,7 +228,7 @@ def tile_attend_gtrace_sq_kernel(tc, xT, wa, wb, us, ts, xx, y, offs, out):
         for c in range(1, TILES):
             scores(sb[c], b_op, c, 0, SLOTS)
         for c in range(TILES):
-            nc.vector.scalar_tensor_tensor(spare[:], sb[c][:], us_xx[:, c:c + 1], h[c][:], MULT, MULT,
+            nc.vector.scalar_tensor_tensor(spare[TILES + c][:], sb[c][:], us_xx[:, c:c + 1], h[c][:], MULT, MULT,
                                            accum_out=acc[:, c:c + 1])
         nc.vector.tensor_tensor(res_cols[:, 0:P:32], acc[:], e[:], SUB)
         res_rows = keep.tile([P, P], F32, name="res_rows", align_bytes=64)

@@ -41,11 +41,12 @@ def tile_attend_gtrace_sq_kernel(tc, xT, wa, wb, us, ts, xx, y, offs, out):
 
         ts_stage = keep.tile([1, T], F32, name="ts_stage")
         nc.sync.dma_start(out=ts_stage[:], in_=ts[0:1, :])
+        nc.sync.dma_start(out=wa_planes[0][:], in_=wa_v[:, 0, :])
         nc.sync.dma_start(offsets[:], offs)
         us_stage = keep.tile([2 * TILES, P], F32, name="us_stage")
         nc.scalar.dma_start(out=us_stage[0:TILES, :], in_=us.rearrange("(c p) o -> c (p o)", p=P))
         nc.scalar.dma_start(out=us_stage[TILES:2 * TILES, :], in_=xx.rearrange("(c p) o -> c (p o)", p=P))
-        for t in range(PACK):
+        for t in range(1, PACK):
             nc.sync.dma_start(out=wa_planes[t][:], in_=wa_v[:, t, :])
         for u in range(2):
             nc.sync.dma_start(out=x_raw[u][:], in_=x_v[:, :, u * HALF:(u + 1) * HALF])
@@ -142,11 +143,11 @@ def tile_attend_gtrace_sq_kernel(tc, xT, wa, wb, us, ts, xx, y, offs, out):
 
         za = [keep.tile([P, SLOTS], F32, name="za%d" % c) for c in range(2)]
         ga = [keep.tile([P, SLOTS], F32, name="ga%d" % c) for c in range(TILES)]
-        h = [keep.tile([P, SLOTS], F32, name="h%d" % c) for c in range(TILES)]
+        h = [keep.tile([P, SLOTS], F32, name="h%d" % c)[:] for c in range(2)]
         spare = [keep.tile([P, SLOTS], F32, name="spare%d" % n) for n in range(2 * TILES)]
         e = keep.tile([P, TILES], F32, name="e")
         acc = keep.tile([P, TILES], F32, name="acc")
-        b_planes = keep.tile([P, 4, PACK, P], BF16, name="b_planes")
+        b_planes = keep.tile([P, PACK, SLOTS], BF16, name="b_planes")
 
         def y_of(c):
             return y_sb[c // 2][:, c % 2, :]
@@ -177,13 +178,14 @@ def tile_attend_gtrace_sq_kernel(tc, xT, wa, wb, us, ts, xx, y, offs, out):
         def weigh_back(u, scaled, names):
             for j in range(2):
                 bank = turn_back(scaled, j, names[j])
-                nc.scalar.copy(out=h[2 * u + j][:], in_=bank[:])
+                nc.scalar.copy(out=h[2 * u + j], in_=bank[:])
 
         def gather_b(t):
-            nc.vector.tensor_copy(b_planes[:, :, t, :], wb_planes[t][:].indirect(offsets[:]))
+            nc.vector.tensor_copy(b_planes[:, t, :], wb_planes[t][:].indirect(offsets[:]))
 
         sa = [psum.tile([P, SLOTS], F32, name="bank%d" % c) for c in range(2)]
-        scores(sa[0], a_op, 0, 0, SLOTS)
+        scores(sa[0], a_op, 0, 0, HALF)
+        scores(sa[0], a_op, 0, HALF, SLOTS)
         scores(sa[1], a_op, 1, 0, SLOTS)
         nc.vector.scalar_tensor_tensor(za[0][:], sa[0][:], usxx[:, 0:1], ts_all[:], MULT, MULT)
         saT = [psum.tile([P, 2, HALF], F32, name="bank%d" % (2 + j)) for j in range(2)]
@@ -205,19 +207,23 @@ def tile_attend_gtrace_sq_kernel(tc, xT, wa, wb, us, ts, xx, y, offs, out):
         hT0 = weigh_turned(0, ("bank6", "bank7"))
         with_targets(0)
         gather_b(0)
+        with_targets(1)
         for j in range(2):
             nc.vector.scalar_tensor_tensor(ga[2 + j][:], u_banks[j][:], usxx[:, 2 + j:3 + j], y_of(2 + j), MULT, SUB)
         hT1 = weigh_turned(1, ("bank2", "bank3"))
         weigh_back(0, hT0, ("bank0", "bank1"))
-        weigh_back(1, hT1, ("bank4", "bank5"))
-        with_targets(1)
+        h_banks = [turn_back(hT1, j, "bank%d" % (4 + j)) for j in range(2)]
         gather_b(1)
         with_targets(2)
         gather_b(2)
         for b in range(4):
-            nc.vector.tensor_copy(b_planes[:, b, 3, :], wb_planes[3][:].indirect(offsets[:, b * 8:(b + 1) * 8]))
+            nc.vector.tensor_copy(b_planes[:, 3, b * P:(b + 1) * P], wb_planes[3][:].indirect(offsets[:, b * 8:(b + 1) * 8]))
         for b in range(4):
-            interleave(nc.scalar.copy if b < 2 else nc.vector.tensor_copy, b_op[0][:, b * P:(b + 1) * P, :], b_planes[:, b, :, :])
+            interleave(nc.scalar.copy if b < 2 else nc.vector.tensor_copy, b_op[0][:, b * P:(b + 1) * P, :], b_planes[:, :, b * P:(b + 1) * P])
+        h_late = keep.tile([P, 2, SLOTS], F32, name="b_planes")
+        for j in range(2):
+            h.append(h_late[:, j, :])
+            nc.scalar.copy(out=h_late[:, j, :], in_=h_banks[j][:])
         quantize(b_op, 0, HALF)
         quantize(b_op, HALF, SLOTS)
         with_targets(3)
@@ -228,7 +234,7 @@ def tile_attend_gtrace_sq_kernel(tc, xT, wa, wb, us, ts, xx, y, offs, out):
         for c in range(1, TILES):
             scores(sb[c], b_op, c, 0, SLOTS)
         for c in range(TILES):
-            nc.vector.scalar_tensor_tensor(spare[TILES + c][:], sb[c][:], us_xx[:, c:c + 1], h[c][:], MULT, MULT,
+            nc.vector.scalar_tensor_tensor(spare[TILES + c][:], sb[c][:], us_xx[:, c:c + 1], h[c], MULT, MULT,
                                            accum_out=acc[:, c:c + 1])
         nc.vector.tensor_tensor(res_cols[:, 0:P:32], acc[:], e[:], SUB)
         res_rows = keep.tile([P, P], F32, name="res_rows", align_bytes=64)

@@ -7,7 +7,9 @@ D, R, SLOTS, T = 512, 512, 512, 2048
 P = 128
 PACK = 4
 TILES = R // P
-HALF = 256
+BLOCKS = SLOTS // P
+HALF = SLOTS // 2
+EARLY = 2
 
 F32 = mybir.dt.float32
 BF16 = mybir.dt.bfloat16
@@ -16,8 +18,10 @@ U16 = mybir.dt.uint16
 U8 = mybir.dt.uint8
 FP8X4 = mybir.dt.float8_e4m3fn_x4
 MULT = mybir.AluOpType.mult
+ADD = mybir.AluOpType.add
 SUB = mybir.AluOpType.subtract
 COPY = mybir.ActivationFunctionType.Copy
+SQUARE = mybir.ActivationFunctionType.Square
 
 FLOPS = 2 * 2 * D * R * SLOTS
 BYTES = 4 * (D * R + 2 * D * T + 2 * R + T + R * SLOTS + R) + 2 * P * SLOTS // 16
@@ -27,31 +31,40 @@ def tile_attend_gtrace_sq_kernel(tc, xT, wa, wb, us, ts, xx, y, offs, out):
     nc = tc.nc
     with ExitStack() as ctx:
         keep = ctx.enter_context(tc.tile_pool(name="keep", bufs=1))
+        shared = ctx.enter_context(tc.tile_pool(name="shared", bufs=1))
         psum = ctx.enter_context(tc.psum_pool(name="psum", bufs=1))
+
+        def bank(n):
+            return psum.tile([P, SLOTS], F32, name="bank%d" % n)
+
+        def scratch(name):
+            return keep.tile([P, SLOTS], F32, name=name)
+
+        def scratch_at(name, offset):
+            return shared.tile([P, SLOTS], F32, name=name, offset=offset)
 
         offsets = keep.tile([P, SLOTS // 16], U16, name="offsets")
         wa_planes = [keep.tile([P, T], F32, name="wa%d" % t) for t in range(PACK)]
         wb_planes = [keep.tile([P, T], F32, name="wb%d" % t) for t in range(PACK)]
-        x_raw = [keep.tile([P, PACK, HALF], F32, name="x_raw%d" % u) for u in range(2)]
-        y_sb = [keep.tile([P, 2, SLOTS], F32, name="y_sb%d" % u) for u in range(2)]
+        x_raw = keep.tile([P, PACK, R], F32, name="x_raw")
+        y_halves = [keep.tile([P, 2, SLOTS], F32, name="y_half%d" % u) for u in range(2)]
+        y_sb = [y_halves[c // 2][:, c % 2, :] for c in range(TILES)]
         wa_v = wa.rearrange("(p t) w -> p t w", t=PACK)
         wb_v = wb.rearrange("(p t) w -> p t w", t=PACK)
-        x_v = xT.rearrange("(p t) r -> p t r", t=PACK)
         y_v = y.rearrange("(c p) i -> p c i", p=P)
 
         ts_stage = keep.tile([1, T], F32, name="ts_stage")
+        us_stage = keep.tile([2 * TILES, P], F32, name="us_stage")
         nc.sync.dma_start(out=ts_stage[:], in_=ts[0:1, :])
         nc.sync.dma_start(out=wa_planes[0][:], in_=wa_v[:, 0, :])
         nc.sync.dma_start(offsets[:], offs)
-        us_stage = keep.tile([2 * TILES, P], F32, name="us_stage")
-        nc.scalar.dma_start(out=us_stage[0:TILES, :], in_=us.rearrange("(c p) o -> c (p o)", p=P))
-        nc.scalar.dma_start(out=us_stage[TILES:2 * TILES, :], in_=xx.rearrange("(c p) o -> c (p o)", p=P))
+        nc.sync.dma_start(out=us_stage[0:TILES, :], in_=us.rearrange("(c p) o -> c (p o)", p=P))
+        nc.sync.dma_start(out=us_stage[TILES:2 * TILES, :], in_=xx.rearrange("(c p) o -> c (p o)", p=P))
         for t in range(1, PACK):
             nc.sync.dma_start(out=wa_planes[t][:], in_=wa_v[:, t, :])
+        nc.sync.dma_start(out=x_raw[:], in_=xT.rearrange("(p t) r -> p t r", t=PACK))
         for u in range(2):
-            nc.sync.dma_start(out=x_raw[u][:], in_=x_v[:, :, u * HALF:(u + 1) * HALF])
-        for u in range(2):
-            nc.sync.dma_start(out=y_sb[u][:], in_=y_v[:, 2 * u:2 * u + 2, :])
+            nc.sync.dma_start(out=y_halves[u][:], in_=y_v[:, 2 * u:2 * u + 2, :])
         for t in range(PACK):
             nc.sync.dma_start(out=wb_planes[t][:], in_=wb_v[:, t, :])
 
@@ -66,44 +79,59 @@ def tile_attend_gtrace_sq_kernel(tc, xT, wa, wb, us, ts, xx, y, offs, out):
         nc.vector.tensor_copy(ts_win[0:1, :], ts_stage[:])
         nc.scalar.activation(row_scales[0:2 * TILES, :], us_stage[:], COPY)
 
-        bank = psum.tile([P, SLOTS], F32, name="bank5")
-        nc.tensor.transpose(bank[:, 0:P], row_scales[:], ident[:])
+        turned = bank(4)
+        nc.tensor.transpose(turned[:, 0:P], row_scales[:], ident[:])
         usxx = keep.tile([P, 2 * TILES], F32, name="usxx")
-        nc.scalar.copy(out=usxx[:], in_=bank[:, 0:2 * TILES])
+        nc.scalar.copy(out=usxx[:], in_=turned[:, 0:2 * TILES])
+        neg = keep.tile([P, 2 * TILES], F32, name="neg")
+        nc.scalar.activation(neg[:], turned[:, 0:2 * TILES], COPY, scale=-1.0)
         us_xx = keep.tile([P, TILES], F32, name="us_xx")
-        nc.vector.tensor_tensor(us_xx[:], usxx[:, 0:TILES], usxx[:, TILES:2 * TILES], MULT)
+        for c in range(TILES):
+            nc.scalar.activation(us_xx[:, c:c + 1], turned[:, c:c + 1], COPY, scale=usxx[:, TILES + c:TILES + c + 1])
 
-        ts_row = keep.tile([P, SLOTS], F32, name="ts_row")
+        def block(ap, b):
+            return ap[:, b * P:(b + 1) * P]
+
+        ts_row = scratch("ts_row")
         nc.vector.tensor_copy(ts_row[:], ts_win[:].indirect(offsets[:]))
-        bank = psum.tile([P, TILES, P], F32, name="bank6")
-        for b in range(4):
-            nc.tensor.transpose(bank[:, b, :], ts_row[:, b * P:(b + 1) * P], ident[:])
-        ts_cols = keep.tile([P, 4], F32, name="ts_cols")
-        nc.scalar.copy(out=ts_cols[:], in_=bank[:, :, 0])
-        bank = psum.tile([P, 4, P], F32, name="bank7")
-        for b in range(4):
-            nc.tensor.transpose(bank[:, b, :], ts_cols[:, b:b + 1].to_broadcast([P, P]), ident[:])
-        ts_all = keep.tile([P, SLOTS], F32, name="ts_all")
-        nc.scalar.copy(out=ts_all[:], in_=bank[:].rearrange("p b m -> p (b m)"))
+        turned = bank(5)
+        for b in range(BLOCKS):
+            nc.tensor.transpose(block(turned, b), block(ts_row, b), ident[:])
+        ts_cols = shared.tile([P, BLOCKS], F32, name="ts_cols", offset=8192)
+        nc.scalar.copy(out=ts_cols[:], in_=turned[:, 0:SLOTS:P])
+        neg_ts_cols = keep.tile([P, BLOCKS], F32, name="neg_ts_cols")
+        nc.scalar.activation(neg_ts_cols[:], turned[:, 0:SLOTS:P], COPY, scale=-1.0)
+        turned = bank(6)
+        for b in range(BLOCKS):
+            nc.tensor.transpose(block(turned, b), ts_cols[:, b:b + 1].to_broadcast([P, P]), ident[:])
+        ts_all = scratch("ts_all")
+        nc.scalar.copy(out=ts_all[:], in_=turned[:])
 
-        def operand(name):
-            grouped = keep.tile([P, SLOTS, PACK], BF16, name=name + "_grouped", align_bytes=64)
+        def operand(name, grouped):
             codes = keep.tile([P, SLOTS], U32, name=name + "_codes", align_bytes=64)
             scales = keep.tile([P, SLOTS], U8, name=name + "_scales", align_bytes=64)
             return grouped, codes, scales
 
-        def quantize(op, c0, c1):
-            grouped, codes, scales = op
+        def quantize(op, c0, c1, grouped):
+            codes, scales = op[1:]
             nc.vector.quantize_mx(
                 out=codes[:, c0:c1].bitcast(FP8X4),
                 scales=scales[:, c0:c1],
-                in_=grouped[:, c0:c1, :].rearrange("p w t -> p (w t)"),
+                in_=grouped.rearrange("p w t -> p (w t)"),
             )
 
-        def gather(op, planes, t, c0, c1):
-            nc.vector.tensor_copy(op[0][:, c0:c1, t], planes[t][:].indirect(offsets[:, c0 // 16:c1 // 16]))
+        def gather_operand(op, planes, pair):
+            for t in range(2):
+                nc.vector.tensor_copy(pair[:, t, :], planes[t][:].indirect(offsets[:]))
+            nc.scalar.copy(out=op[0][:, :, 0:2], in_=pair[:].rearrange("p t s -> p s t"))
+            nc.vector.tensor_copy(op[0][:, :, 2], planes[2][:].indirect(offsets[:]))
+            for c0 in (0, HALF):
+                nc.vector.tensor_copy(op[0][:, c0:c0 + HALF, 3],
+                                      planes[3][:].indirect(offsets[:, c0 // 16:(c0 + HALF) // 16]))
+            for c0 in (0, HALF):
+                quantize(op, c0, c0 + HALF, op[0][:, c0:c0 + HALF, :])
 
-        def scores(dst, w_op, c, c0, c1):
+        def scores(dst, w_op, c, c0, c1, start, stop):
             rows = slice(c * P, (c + 1) * P)
             nc.tensor.matmul_mx(
                 out=dst[:, c0:c1],
@@ -111,132 +139,93 @@ def tile_attend_gtrace_sq_kernel(tc, xT, wa, wb, us, ts, xx, y, offs, out):
                 lhsT_scale=x_op[2][:, rows],
                 rhs=w_op[1][:, c0:c1].bitcast(FP8X4),
                 rhs_scale=w_op[2][:, c0:c1],
-                start=True,
-                stop=True,
+                start=start,
+                stop=stop,
             )
 
-        x_op = operand("x")
-        a_op = operand("a")
-        b_op = operand("b")
+        def turn(dst, src, start, stop):
+            for b in range(BLOCKS):
+                nc.tensor.matmul(block(dst, b), block(src, b), ident[:], start=start and b == 0,
+                                 stop=stop and b == BLOCKS - 1, is_transpose=True)
 
-        def interleave(copy, grouped, planes):
-            copy(out=grouped.rearrange("p (c i) t -> p c t i", i=4), in_=planes.rearrange("p t (c i) -> p c t i", i=4))
+        x_op = operand("x", None)
+        a_op = operand("a", keep.tile([P, SLOTS, PACK], BF16, name="a_grouped", align_bytes=64))
 
-        def interleave_x(copy, c):
-            interleave(copy, x_op[0][:, c * P:(c + 1) * P, :], x_raw[c // 2][:, :, (c % 2) * P:(c % 2 + 1) * P])
-
-        a_pair = keep.tile([P, 2, SLOTS], BF16, name="a_pair")
-        for t in range(2):
-            nc.vector.tensor_copy(a_pair[:, t, :], wa_planes[t][:].indirect(offsets[:]))
-        nc.scalar.copy(out=a_op[0][:, :, 0:2], in_=a_pair[:].rearrange("p t s -> p s t"))
-        gather(a_op, wa_planes, 2, 0, SLOTS)
-        gather(a_op, wa_planes, 3, 0, HALF)
-        gather(a_op, wa_planes, 3, HALF, SLOTS)
-        for c in range(3):
-            interleave_x(nc.scalar.copy, c)
-        quantize(a_op, 0, HALF)
-        quantize(a_op, HALF, SLOTS)
-        quantize(x_op, 0, P)
-        quantize(x_op, P, HALF)
-        interleave_x(nc.vector.tensor_copy, 3)
-        quantize(x_op, HALF, R)
-
-        za = [keep.tile([P, SLOTS], F32, name="za%d" % c) for c in range(2)]
-        ga = [keep.tile([P, SLOTS], F32, name="ga%d" % c) for c in range(TILES)]
-        h = [keep.tile([P, SLOTS], F32, name="h%d" % c)[:] for c in range(2)]
-        spare = [keep.tile([P, SLOTS], F32, name="spare%d" % n) for n in range(2 * TILES)]
-        e = keep.tile([P, TILES], F32, name="e")
-        acc = keep.tile([P, TILES], F32, name="acc")
-        b_planes = keep.tile([P, PACK, SLOTS], BF16, name="b_planes")
-
-        def y_of(c):
-            return y_sb[c // 2][:, c % 2, :]
-
-        def with_targets(c):
-            nc.vector.scalar_tensor_tensor(spare[c][:], ga[c][:], usxx[:, TILES + c:TILES + c + 1], y_of(c),
-                                           MULT, MULT, accum_out=e[:, c:c + 1])
-
-        def scale_slots(banks, name):
-            scaled = keep.tile([P, 4, HALF], F32, name=name)
-            for b in range(4):
-                nc.scalar.activation(scaled[:, b, :], banks[b // 2][:, b % 2, :], COPY, scale=ts_cols[:, b:b + 1])
-            return scaled
-
-        def turn_back(scaled, j, name):
-            bank = psum.tile([P, SLOTS], F32, name=name)
-            for b in range(4):
-                nc.tensor.transpose(bank[:, b * P:(b + 1) * P], scaled[:, b, j * P:(j + 1) * P], ident[:])
-            return bank
-
-        def weigh_turned(u, names):
-            banks = [psum.tile([P, 2, HALF], F32, name=n) for n in names]
-            for b in range(4):
-                for j in range(2):
-                    nc.tensor.transpose(banks[b // 2][:, b % 2, j * P:(j + 1) * P], ga[2 * u + j][:, b * P:(b + 1) * P], ident[:])
-            return scale_slots(banks, "hT%d" % u)
-
-        def weigh_back(u, scaled, names):
-            for j in range(2):
-                bank = turn_back(scaled, j, names[j])
-                nc.scalar.copy(out=h[2 * u + j], in_=bank[:])
-
-        def gather_b(t):
-            nc.vector.tensor_copy(b_planes[:, t, :], wb_planes[t][:].indirect(offsets[:]))
-
-        sa = [psum.tile([P, SLOTS], F32, name="bank%d" % c) for c in range(2)]
-        scores(sa[0], a_op, 0, 0, HALF)
-        scores(sa[0], a_op, 0, HALF, SLOTS)
-        scores(sa[1], a_op, 1, 0, SLOTS)
-        nc.vector.scalar_tensor_tensor(za[0][:], sa[0][:], usxx[:, 0:1], ts_all[:], MULT, MULT)
-        saT = [psum.tile([P, 2, HALF], F32, name="bank%d" % (2 + j)) for j in range(2)]
-        for b in range(4):
-            nc.tensor.matmul_mx(
-                out=saT[b // 2][:, b % 2, :],
-                lhsT=a_op[1][:, b * P:(b + 1) * P].bitcast(FP8X4),
-                lhsT_scale=a_op[2][:, b * P:(b + 1) * P],
-                rhs=x_op[1][:, HALF:R].bitcast(FP8X4),
-                rhs_scale=x_op[2][:, HALF:R],
-                start=True,
-                stop=True,
-            )
-        uT = scale_slots(saT, "uT")
-        u_banks = [turn_back(uT, j, "bank%d" % (4 + j)) for j in range(2)]
-        nc.vector.scalar_tensor_tensor(za[1][:], sa[1][:], usxx[:, 1:2], ts_all[:], MULT, MULT)
-        for c in range(2):
-            nc.vector.tensor_tensor(ga[c][:], za[c][:], y_of(c), SUB)
-        hT0 = weigh_turned(0, ("bank6", "bank7"))
-        with_targets(0)
-        gather_b(0)
-        with_targets(1)
-        for j in range(2):
-            nc.vector.scalar_tensor_tensor(ga[2 + j][:], u_banks[j][:], usxx[:, 2 + j:3 + j], y_of(2 + j), MULT, SUB)
-        hT1 = weigh_turned(1, ("bank2", "bank3"))
-        weigh_back(0, hT0, ("bank0", "bank1"))
-        h_banks = [turn_back(hT1, j, "bank%d" % (4 + j)) for j in range(2)]
-        gather_b(1)
-        with_targets(2)
-        gather_b(2)
-        for b in range(4):
-            nc.vector.tensor_copy(b_planes[:, 3, b * P:(b + 1) * P], wb_planes[3][:].indirect(offsets[:, b * 8:(b + 1) * 8]))
-        for b in range(4):
-            interleave(nc.scalar.copy if b < 2 else nc.vector.tensor_copy, b_op[0][:, b * P:(b + 1) * P, :], b_planes[:, :, b * P:(b + 1) * P])
-        h_late = keep.tile([P, 2, SLOTS], F32, name="b_planes")
-        for j in range(2):
-            h.append(h_late[:, j, :])
-            nc.scalar.copy(out=h_late[:, j, :], in_=h_banks[j][:])
-        quantize(b_op, 0, HALF)
-        quantize(b_op, HALF, SLOTS)
-        with_targets(3)
-
-        sb = [psum.tile([P, SLOTS], F32, name="bank%d" % n) for n in (6, 7, 0, 1)]
-        scores(sb[0], b_op, 0, 0, HALF)
-        scores(sb[0], b_op, 0, HALF, SLOTS)
-        for c in range(1, TILES):
-            scores(sb[c], b_op, c, 0, SLOTS)
+        gather_operand(a_op, wa_planes, shared.tile([P, 2, SLOTS], BF16, name="a_pair", offset=12288))
+        x_grouped = [shared.tile([P, P, PACK], BF16, name="x_first", align_bytes=64, offset=12288),
+                     shared.tile([P, R - P, PACK], BF16, name="x_rest", align_bytes=64, offset=6144)]
+        x_tiles = [x_grouped[0][:]] + [x_grouped[1][:, c * P:(c + 1) * P, :] for c in range(TILES - 1)]
         for c in range(TILES):
-            nc.vector.scalar_tensor_tensor(spare[TILES + c][:], sb[c][:], us_xx[:, c:c + 1], h[c], MULT, MULT,
-                                           accum_out=acc[:, c:c + 1])
-        nc.vector.tensor_tensor(res_cols[:, 0:P:32], acc[:], e[:], SUB)
+            copy = nc.vector.tensor_copy if c < 1 else nc.scalar.copy
+            copy(out=x_tiles[c].rearrange("p (c i) t -> p c t i", i=4),
+                 in_=x_raw[:, :, c * P:(c + 1) * P].rearrange("p t (c i) -> p c t i", i=4))
+        for c in range(TILES):
+            quantize(x_op, c * P, (c + 1) * P, x_tiles[c])
+
+        neg_za = [scratch_at("neg_za0", 16384), scratch_at("neg_za1", 2048), scratch("neg_za2"), scratch("neg_za3")]
+        for c in range(TILES):
+            sa = bank(c)
+            scores(sa, a_op, c, 0, SLOTS, True, True)
+            nc.vector.scalar_tensor_tensor(neg_za[c][:], sa[:], neg[:, c:c + 1], ts_all[:], MULT, MULT)
+
+        xx_cols = usxx[:, TILES:2 * TILES]
+        cross = keep.tile([P, TILES], F32, name="cross")
+        y_sq = keep.tile([P, TILES], F32, name="y_sq")
+        rest = keep.tile([P, TILES], F32, name="rest")
+        acc = keep.tile([P, TILES], F32, name="acc")
+        weights = [scratch("weights%d" % c) for c in range(TILES)]
+
+        def scale_turned(scaled, residual):
+            for b in range(BLOCKS):
+                nc.scalar.activation(block(scaled, b), block(residual, b), COPY, scale=neg_ts_cols[:, b:b + 1])
+
+        def turn_back(c, scaled, back):
+            turn(back, scaled, True, True)
+            nc.scalar.copy(out=weights[c][:], in_=back[:])
+
+        def square_targets(c, unused):
+            nc.scalar.activation(unused[:], y_sb[c], SQUARE, accum_out=y_sq[:, c:c + 1])
+
+        for c in range(EARLY):
+            square_targets(c, scratch_at("y_sq%d" % c, 10752 + 2048 * c))
+
+        scaled = []
+        for c0 in (0, 2):
+            for c in (c0, c0 + 1):
+                residual = bank((4 + c) if c < 2 else c - 2)
+                turn(residual, neg_za[c], True, False)
+                turn(residual, y_sb[c], False, True)
+                scaled.append(scratch("scaled%d" % c))
+                scale_turned(scaled[c], residual)
+            for c in (c0, c0 + 1):
+                turn_back(c, scaled[c], bank((6 + c) if c < 2 else c + 2))
+        for c in range(EARLY):
+            nc.vector.scalar_tensor_tensor(scratch("cross%d" % c)[:], neg_za[c][:], -1.0, y_sb[c],
+                                           MULT, MULT, accum_out=cross[:, c:c + 1])
+
+        both = [bank(c) for c in range(EARLY, TILES)]
+        for c in range(EARLY, TILES):
+            scores(both[c - EARLY], a_op, c, 0, SLOTS, True, False)
+        b_op = operand("b", shared.tile([P, SLOTS, PACK], BF16, name="b_grouped", align_bytes=64, offset=16384))
+        gather_operand(b_op, wb_planes, shared.tile([P, 2, SLOTS], BF16, name="b_pair", offset=2048))
+        sb = [bank(1), bank(0)] + both
+        scores(sb[0], b_op, 0, 0, HALF, True, True)
+        scores(sb[0], b_op, 0, HALF, SLOTS, True, True)
+        scores(sb[1], b_op, 1, 0, SLOTS, True, True)
+        for c in range(EARLY, TILES):
+            scores(sb[c], b_op, c, 0, SLOTS, False, True)
+        for c in range(EARLY, TILES):
+            nc.scalar.activation(scratch_at("cross%d" % c, 2048 * c - 3072)[:], neg_za[c][:], SQUARE,
+                                 accum_out=cross[:, c:c + 1])
+        for c in range(EARLY, TILES):
+            square_targets(c, scratch_at("y_sq%d" % c, 2048 * c - 3072))
+        nc.gpsimd.tensor_tensor(rest[:], y_sq[:], cross[:], SUB)
+        xx_rest = keep.tile([P, TILES], F32, name="xx_rest")
+        nc.gpsimd.tensor_tensor(xx_rest[:], rest[:], xx_cols, MULT)
+        for c in range(TILES):
+            nc.vector.scalar_tensor_tensor(scratch("last%d" % c)[:], sb[c][:], us_xx[:, c:c + 1], weights[c][:],
+                                           MULT, MULT, accum_out=acc[:, c:c + 1])
+        nc.vector.tensor_tensor(res_cols[:, 0:P:32], acc[:], xx_rest[:], ADD)
         res_rows = keep.tile([P, P], F32, name="res_rows", align_bytes=64)
         nc.vector.transpose(res_rows[:], res_cols[:])
         nc.sync.dma_start(

@@ -9,7 +9,6 @@ PACK = 4
 TILES = R // P
 BLOCKS = SLOTS // P
 HALF = SLOTS // 2
-EARLY = 2
 
 F32 = mybir.dt.float32
 BF16 = mybir.dt.bfloat16
@@ -47,8 +46,8 @@ def tile_attend_gtrace_sq_kernel(tc, xT, wa, wb, us, ts, xx, y, offs, out):
         wa_planes = [keep.tile([P, T], F32, name="wa%d" % t) for t in range(PACK)]
         wb_planes = [keep.tile([P, T], F32, name="wb%d" % t) for t in range(PACK)]
         x_raw = keep.tile([P, PACK, R], F32, name="x_raw")
-        y_halves = [keep.tile([P, 2, SLOTS], F32, name="y_half%d" % u) for u in range(2)]
-        y_sb = [y_halves[c // 2][:, c % 2, :] for c in range(TILES)]
+        y_all = shared.tile([P, TILES, SLOTS], F32, name="y_all", offset=2048)
+        y_sb = [y_all[:, c, :] for c in range(TILES)]
         wa_v = wa.rearrange("(p t) w -> p t w", t=PACK)
         wb_v = wb.rearrange("(p t) w -> p t w", t=PACK)
         y_v = y.rearrange("(c p) i -> p c i", p=P)
@@ -64,7 +63,7 @@ def tile_attend_gtrace_sq_kernel(tc, xT, wa, wb, us, ts, xx, y, offs, out):
             nc.sync.dma_start(out=wa_planes[t][:], in_=wa_v[:, t, :])
         nc.sync.dma_start(out=x_raw[:], in_=xT.rearrange("(p t) r -> p t r", t=PACK))
         for u in range(2):
-            nc.sync.dma_start(out=y_halves[u][:], in_=y_v[:, 2 * u:2 * u + 2, :])
+            nc.sync.dma_start(out=y_all[:, 2 * u:2 * u + 2, :], in_=y_v[:, 2 * u:2 * u + 2, :])
         for t in range(PACK):
             nc.sync.dma_start(out=wb_planes[t][:], in_=wb_v[:, t, :])
 
@@ -83,8 +82,8 @@ def tile_attend_gtrace_sq_kernel(tc, xT, wa, wb, us, ts, xx, y, offs, out):
         nc.tensor.transpose(turned[:, 0:P], row_scales[:], ident[:])
         usxx = keep.tile([P, 2 * TILES], F32, name="usxx")
         nc.scalar.copy(out=usxx[:], in_=turned[:, 0:2 * TILES])
-        neg = keep.tile([P, 2 * TILES], F32, name="neg")
-        nc.scalar.activation(neg[:], turned[:, 0:2 * TILES], COPY, scale=-1.0)
+        half_xx = keep.tile([P, TILES], F32, name="half_xx")
+        nc.scalar.activation(half_xx[:], turned[:, TILES:2 * TILES], COPY, scale=0.5)
         us_xx = keep.tile([P, TILES], F32, name="us_xx")
         for c in range(TILES):
             nc.scalar.activation(us_xx[:, c:c + 1], turned[:, c:c + 1], COPY, scale=usxx[:, TILES + c:TILES + c + 1])
@@ -97,10 +96,8 @@ def tile_attend_gtrace_sq_kernel(tc, xT, wa, wb, us, ts, xx, y, offs, out):
         turned = bank(5)
         for b in range(BLOCKS):
             nc.tensor.transpose(block(turned, b), block(ts_row, b), ident[:])
-        ts_cols = shared.tile([P, BLOCKS], F32, name="ts_cols", offset=8192)
+        ts_cols = shared.tile([P, BLOCKS], F32, name="ts_cols", offset=22528)
         nc.scalar.copy(out=ts_cols[:], in_=turned[:, 0:SLOTS:P])
-        neg_ts_cols = keep.tile([P, BLOCKS], F32, name="neg_ts_cols")
-        nc.scalar.activation(neg_ts_cols[:], turned[:, 0:SLOTS:P], COPY, scale=-1.0)
         turned = bank(6)
         for b in range(BLOCKS):
             nc.tensor.transpose(block(turned, b), ts_cols[:, b:b + 1].to_broadcast([P, P]), ident[:])
@@ -143,17 +140,12 @@ def tile_attend_gtrace_sq_kernel(tc, xT, wa, wb, us, ts, xx, y, offs, out):
                 stop=stop,
             )
 
-        def turn(dst, src, start, stop):
-            for b in range(BLOCKS):
-                nc.tensor.matmul(block(dst, b), block(src, b), ident[:], start=start and b == 0,
-                                 stop=stop and b == BLOCKS - 1, is_transpose=True)
-
         x_op = operand("x", None)
         a_op = operand("a", keep.tile([P, SLOTS, PACK], BF16, name="a_grouped", align_bytes=64))
 
-        gather_operand(a_op, wa_planes, shared.tile([P, 2, SLOTS], BF16, name="a_pair", offset=12288))
-        x_grouped = [shared.tile([P, P, PACK], BF16, name="x_first", align_bytes=64, offset=12288),
-                     shared.tile([P, R - P, PACK], BF16, name="x_rest", align_bytes=64, offset=6144)]
+        gather_operand(a_op, wa_planes, shared.tile([P, 2, SLOTS], BF16, name="a_pair", offset=13312))
+        x_grouped = [shared.tile([P, P, PACK], BF16, name="x_first", align_bytes=64, offset=13312),
+                     shared.tile([P, R - P, PACK], BF16, name="x_rest", align_bytes=64, offset=20480)]
         x_tiles = [x_grouped[0][:]] + [x_grouped[1][:, c * P:(c + 1) * P, :] for c in range(TILES - 1)]
         for c in range(TILES):
             copy = nc.vector.tensor_copy if c < 1 else nc.scalar.copy
@@ -162,70 +154,44 @@ def tile_attend_gtrace_sq_kernel(tc, xT, wa, wb, us, ts, xx, y, offs, out):
         for c in range(TILES):
             quantize(x_op, c * P, (c + 1) * P, x_tiles[c])
 
-        neg_za = [scratch_at("neg_za0", 16384), scratch_at("neg_za1", 2048), scratch("neg_za2"), scratch("neg_za3")]
+        squares = keep.tile([P, 3, TILES], F32, name="squares")
+        acc = keep.tile([P, TILES], F32, name="acc")
+
+        def square(kind, c, src, unused):
+            nc.scalar.activation(unused[:], src, SQUARE, accum_out=squares[:, kind, c:c + 1])
+
+        for c in range(TILES):
+            square(0, c, y_sb[c], scratch_at("y_sq%d" % c, 11776 + 2048 * (c % 2)))
+        za = [scratch_at("za0", 16384)] + [scratch("za%d" % c) for c in range(1, TILES)]
         for c in range(TILES):
             sa = bank(c)
             scores(sa, a_op, c, 0, SLOTS, True, True)
-            nc.vector.scalar_tensor_tensor(neg_za[c][:], sa[:], neg[:, c:c + 1], ts_all[:], MULT, MULT)
+            nc.vector.scalar_tensor_tensor(za[c][:], sa[:], usxx[:, c:c + 1], ts_all[:], MULT, MULT)
+            square(1, c, za[c][:], scratch("za_sq%d" % (c % 2)))
+        ga = [scratch("ga%d" % c) for c in range(TILES)]
+        for c in range(TILES):
+            nc.vector.tensor_tensor(ga[c][:], za[c][:], y_sb[c], SUB)
+        weights = [scratch_at("weights%d" % c, 3072 + 2048 * c) for c in range(TILES)]
+        for c in range(TILES):
+            nc.gpsimd.tensor_tensor(weights[c][:], ga[c][:], ts_all[:], MULT)
 
-        xx_cols = usxx[:, TILES:2 * TILES]
-        cross = keep.tile([P, TILES], F32, name="cross")
-        y_sq = keep.tile([P, TILES], F32, name="y_sq")
-        rest = keep.tile([P, TILES], F32, name="rest")
-        acc = keep.tile([P, TILES], F32, name="acc")
-        weights = [scratch("weights%d" % c) for c in range(TILES)]
-
-        def scale_turned(scaled, residual):
-            for b in range(BLOCKS):
-                nc.scalar.activation(block(scaled, b), block(residual, b), COPY, scale=neg_ts_cols[:, b:b + 1])
-
-        def turn_back(c, scaled, back):
-            turn(back, scaled, True, True)
-            nc.scalar.copy(out=weights[c][:], in_=back[:])
-
-        def square_targets(c, unused):
-            nc.scalar.activation(unused[:], y_sb[c], SQUARE, accum_out=y_sq[:, c:c + 1])
-
-        for c in range(EARLY):
-            square_targets(c, scratch_at("y_sq%d" % c, 10752 + 2048 * c))
-
-        scaled = []
-        for c0 in (0, 2):
-            for c in (c0, c0 + 1):
-                residual = bank((4 + c) if c < 2 else c - 2)
-                turn(residual, neg_za[c], True, False)
-                turn(residual, y_sb[c], False, True)
-                scaled.append(scratch("scaled%d" % c))
-                scale_turned(scaled[c], residual)
-            for c in (c0, c0 + 1):
-                turn_back(c, scaled[c], bank((6 + c) if c < 2 else c + 2))
-        for c in range(EARLY):
-            nc.vector.scalar_tensor_tensor(scratch("cross%d" % c)[:], neg_za[c][:], -1.0, y_sb[c],
-                                           MULT, MULT, accum_out=cross[:, c:c + 1])
-
-        both = [bank(c) for c in range(EARLY, TILES)]
-        for c in range(EARLY, TILES):
-            scores(both[c - EARLY], a_op, c, 0, SLOTS, True, False)
         b_op = operand("b", shared.tile([P, SLOTS, PACK], BF16, name="b_grouped", align_bytes=64, offset=16384))
-        gather_operand(b_op, wb_planes, shared.tile([P, 2, SLOTS], BF16, name="b_pair", offset=2048))
-        sb = [bank(1), bank(0)] + both
+        gather_operand(b_op, wb_planes, shared.tile([P, 2, SLOTS], BF16, name="b_pair", offset=1024))
+        sb = [bank(4 + c) for c in range(TILES)]
         scores(sb[0], b_op, 0, 0, HALF, True, True)
         scores(sb[0], b_op, 0, HALF, SLOTS, True, True)
-        scores(sb[1], b_op, 1, 0, SLOTS, True, True)
-        for c in range(EARLY, TILES):
-            scores(sb[c], b_op, c, 0, SLOTS, False, True)
-        for c in range(EARLY, TILES):
-            nc.scalar.activation(scratch_at("cross%d" % c, 2048 * c - 3072)[:], neg_za[c][:], SQUARE,
-                                 accum_out=cross[:, c:c + 1])
-        for c in range(EARLY, TILES):
-            square_targets(c, scratch_at("y_sq%d" % c, 2048 * c - 3072))
-        nc.gpsimd.tensor_tensor(rest[:], y_sq[:], cross[:], SUB)
-        xx_rest = keep.tile([P, TILES], F32, name="xx_rest")
-        nc.gpsimd.tensor_tensor(xx_rest[:], rest[:], xx_cols, MULT)
+        for c in range(1, TILES):
+            scores(sb[c], b_op, c, 0, SLOTS, True, True)
+        for c in range(TILES):
+            square(2, c, ga[c][:], scratch_at("ga_sq%d" % c, 0))
+        rest = keep.tile([P, 3, TILES], F32, name="rest")
+        nc.gpsimd.tensor_tensor(rest[:, 0, :], squares[:, 0, :], squares[:, 1, :], SUB)
+        nc.gpsimd.tensor_tensor(rest[:, 1, :], rest[:, 0, :], squares[:, 2, :], ADD)
+        nc.gpsimd.tensor_tensor(rest[:, 2, :], rest[:, 1, :], half_xx[:], MULT)
         for c in range(TILES):
             nc.vector.scalar_tensor_tensor(scratch("last%d" % c)[:], sb[c][:], us_xx[:, c:c + 1], weights[c][:],
                                            MULT, MULT, accum_out=acc[:, c:c + 1])
-        nc.vector.tensor_tensor(res_cols[:, 0:P:32], acc[:], xx_rest[:], ADD)
+        nc.vector.tensor_tensor(res_cols[:, 0:P:32], acc[:], rest[:, 2, :], ADD)
         res_rows = keep.tile([P, P], F32, name="res_rows", align_bytes=64)
         nc.vector.transpose(res_rows[:], res_cols[:])
         nc.sync.dma_start(

@@ -46,7 +46,7 @@ def tile_attend_gtrace_sq_kernel(tc, xT, wa, wb, us, ts, xx, y, offs, out):
         wa_planes = [keep.tile([P, T], F32, name="wa%d" % t) for t in range(PACK)]
         wb_planes = [keep.tile([P, T], F32, name="wb%d" % t) for t in range(PACK)]
         x_raw = keep.tile([P, PACK, R], F32, name="x_raw")
-        y_all = shared.tile([P, TILES, SLOTS], F32, name="y_all", offset=2048)
+        y_all = keep.tile([P, TILES, SLOTS], F32, name="y_all")
         y_sb = [y_all[:, c, :] for c in range(TILES)]
         wa_v = wa.rearrange("(p t) w -> p t w", t=PACK)
         wb_v = wb.rearrange("(p t) w -> p t w", t=PACK)
@@ -80,13 +80,15 @@ def tile_attend_gtrace_sq_kernel(tc, xT, wa, wb, us, ts, xx, y, offs, out):
 
         turned = bank(4)
         nc.tensor.transpose(turned[:, 0:P], row_scales[:], ident[:])
-        usxx = keep.tile([P, 2 * TILES], F32, name="usxx")
-        nc.scalar.copy(out=usxx[:], in_=turned[:, 0:2 * TILES])
+        us_cols = shared.tile([P, TILES], F32, name="us_cols", offset=1024)
+        nc.scalar.copy(out=us_cols[:], in_=turned[:, 0:TILES])
+        xx_cols = keep.tile([P, TILES], F32, name="xx_cols")
+        nc.scalar.copy(out=xx_cols[:], in_=turned[:, TILES:2 * TILES])
         half_xx = keep.tile([P, TILES], F32, name="half_xx")
         nc.scalar.activation(half_xx[:], turned[:, TILES:2 * TILES], COPY, scale=0.5)
         us_xx = keep.tile([P, TILES], F32, name="us_xx")
         for c in range(TILES):
-            nc.scalar.activation(us_xx[:, c:c + 1], turned[:, c:c + 1], COPY, scale=usxx[:, TILES + c:TILES + c + 1])
+            nc.scalar.activation(us_xx[:, c:c + 1], turned[:, c:c + 1], COPY, scale=xx_cols[:, c:c + 1])
 
         def block(ap, b):
             return ap[:, b * P:(b + 1) * P]
@@ -166,12 +168,12 @@ def tile_attend_gtrace_sq_kernel(tc, xT, wa, wb, us, ts, xx, y, offs, out):
         for c in range(TILES):
             sa = bank(c)
             scores(sa, a_op, c, 0, SLOTS, True, True)
-            nc.vector.scalar_tensor_tensor(za[c][:], sa[:], usxx[:, c:c + 1], ts_all[:], MULT, MULT)
+            nc.vector.scalar_tensor_tensor(za[c][:], sa[:], us_cols[:, c:c + 1], ts_all[:], MULT, MULT)
             square(1, c, za[c][:], scratch("za_sq%d" % (c % 2)))
         ga = [scratch("ga%d" % c) for c in range(TILES)]
+        weights = [scratch("weights%d" % c) for c in range(TILES)]
         for c in range(TILES):
-            nc.vector.tensor_tensor(ga[c][:], za[c][:], y_sb[c], SUB)
-        weights = [scratch_at("weights%d" % c, 3072 + 2048 * c) for c in range(TILES)]
+            nc.gpsimd.tensor_tensor(ga[c][:], za[c][:], y_sb[c], SUB)
         for c in range(TILES):
             nc.gpsimd.tensor_tensor(weights[c][:], ga[c][:], ts_all[:], MULT)
 

@@ -46,8 +46,8 @@ def tile_attend_gtrace_sq_kernel(tc, xT, wa, wb, us, ts, xx, y, offs, out):
         wa_planes = [keep.tile([P, T], F32, name="wa%d" % t) for t in range(PACK)]
         wb_planes = [keep.tile([P, T], F32, name="wb%d" % t) for t in range(PACK)]
         x_raw = keep.tile([P, PACK, R], F32, name="x_raw")
-        y_all = keep.tile([P, TILES, SLOTS], F32, name="y_all")
-        y_sb = [y_all[:, c, :] for c in range(TILES)]
+        y_pair = keep.tile([P, 2, SLOTS], F32, name="y_pair")
+        y_sb = [y_pair[:, 0, :], y_pair[:, 1, :], scratch_at("y2", 16384)[:], scratch("y3")[:]]
         wa_v = wa.rearrange("(p t) w -> p t w", t=PACK)
         wb_v = wb.rearrange("(p t) w -> p t w", t=PACK)
         y_v = y.rearrange("(c p) i -> p c i", p=P)
@@ -62,10 +62,11 @@ def tile_attend_gtrace_sq_kernel(tc, xT, wa, wb, us, ts, xx, y, offs, out):
         for t in range(1, PACK):
             nc.sync.dma_start(out=wa_planes[t][:], in_=wa_v[:, t, :])
         nc.sync.dma_start(out=x_raw[:], in_=xT.rearrange("(p t) r -> p t r", t=PACK))
-        for u in range(2):
-            nc.sync.dma_start(out=y_all[:, 2 * u:2 * u + 2, :], in_=y_v[:, 2 * u:2 * u + 2, :])
+        nc.sync.dma_start(out=y_pair[:], in_=y_v[:, 0:2, :])
+        nc.sync.dma_start(out=y_sb[2], in_=y_v[:, 2, :])
         for t in range(PACK):
             nc.sync.dma_start(out=wb_planes[t][:], in_=wb_v[:, t, :])
+        nc.sync.dma_start(out=y_sb[3], in_=y_v[:, 3, :])
 
         ts_win = keep.tile([P, T], F32, name="ts_win")
         row_scales = keep.tile([P, P], F32, name="row_scales")
@@ -80,8 +81,10 @@ def tile_attend_gtrace_sq_kernel(tc, xT, wa, wb, us, ts, xx, y, offs, out):
 
         turned = bank(4)
         nc.tensor.transpose(turned[:, 0:P], row_scales[:], ident[:])
-        us_cols = shared.tile([P, TILES], F32, name="us_cols", offset=1024)
-        nc.scalar.copy(out=us_cols[:], in_=turned[:, 0:TILES])
+        us_low = shared.tile([P, 2], F32, name="us_low", offset=1024)
+        nc.scalar.copy(out=us_low[:], in_=turned[:, 0:2])
+        us_high = keep.tile([P, 2], F32, name="us_high")
+        nc.scalar.copy(out=us_high[:], in_=turned[:, 2:TILES])
         xx_cols = keep.tile([P, TILES], F32, name="xx_cols")
         nc.scalar.copy(out=xx_cols[:], in_=turned[:, TILES:2 * TILES])
         half_xx = keep.tile([P, TILES], F32, name="half_xx")
@@ -100,6 +103,8 @@ def tile_attend_gtrace_sq_kernel(tc, xT, wa, wb, us, ts, xx, y, offs, out):
             nc.tensor.transpose(block(turned, b), block(ts_row, b), ident[:])
         ts_cols = shared.tile([P, BLOCKS], F32, name="ts_cols", offset=22528)
         nc.scalar.copy(out=ts_cols[:], in_=turned[:, 0:SLOTS:P])
+        ts_scale = keep.tile([P, BLOCKS], F32, name="ts_scale")
+        nc.scalar.copy(out=ts_scale[:], in_=turned[:, 0:SLOTS:P])
         turned = bank(6)
         for b in range(BLOCKS):
             nc.tensor.transpose(block(turned, b), ts_cols[:, b:b + 1].to_broadcast([P, P]), ident[:])
@@ -159,33 +164,60 @@ def tile_attend_gtrace_sq_kernel(tc, xT, wa, wb, us, ts, xx, y, offs, out):
         squares = keep.tile([P, 3, TILES], F32, name="squares")
         acc = keep.tile([P, TILES], F32, name="acc")
 
-        def square(kind, c, src, unused):
-            nc.scalar.activation(unused[:], src, SQUARE, accum_out=squares[:, kind, c:c + 1])
+        def square(kind, c, src, unused, scale=1.0):
+            nc.scalar.activation(unused[:], src, SQUARE, scale=scale, accum_out=squares[:, kind, c:c + 1])
 
-        for c in range(TILES):
+        for c in range(3):
             square(0, c, y_sb[c], scratch_at("y_sq%d" % c, 11776 + 2048 * (c % 2)))
-        za = [scratch_at("za0", 16384)] + [scratch("za%d" % c) for c in range(1, TILES)]
-        for c in range(TILES):
+        ga = [scratch("ga%d" % c) for c in range(3)]
+        weights = [scratch("weights%d" % c) for c in range(TILES)]
+        za = [scratch("za%d" % c) for c in range(2)]
+        for c in range(2):
             sa = bank(c)
             scores(sa, a_op, c, 0, SLOTS, True, True)
-            nc.vector.scalar_tensor_tensor(za[c][:], sa[:], us_cols[:, c:c + 1], ts_all[:], MULT, MULT)
-            square(1, c, za[c][:], scratch("za_sq%d" % (c % 2)))
-        ga = [scratch("ga%d" % c) for c in range(TILES)]
-        weights = [scratch("weights%d" % c) for c in range(TILES)]
-        for c in range(TILES):
+            nc.vector.scalar_tensor_tensor(za[c][:], sa[:], us_low[:, c:c + 1], ts_all[:], MULT, MULT)
+        turned_scores = [psum.tile([P, 2, HALF], F32, name="bank%d" % (2 + j)) for j in range(2)]
+        scaled = keep.tile([P, BLOCKS, HALF], F32, name="scaled")
+        for b in range(BLOCKS):
+            nc.tensor.matmul_mx(
+                out=turned_scores[b // 2][:, b % 2, :],
+                lhsT=block(a_op[1], b).bitcast(FP8X4),
+                lhsT_scale=block(a_op[2], b),
+                rhs=x_op[1][:, HALF:R].bitcast(FP8X4),
+                rhs_scale=x_op[2][:, HALF:R],
+                start=True,
+                stop=True,
+            )
+        for b in range(BLOCKS):
+            nc.scalar.activation(scaled[:, b, :], turned_scores[b // 2][:, b % 2, :], COPY, scale=ts_scale[:, b:b + 1])
+        ts_sa = [bank(4 + j) for j in range(2)]
+        for j in range(2):
+            for b in range(BLOCKS):
+                nc.tensor.transpose(block(ts_sa[j], b), scaled[:, b, j * P:(j + 1) * P], ident[:])
+        for c in range(2):
             nc.gpsimd.tensor_tensor(ga[c][:], za[c][:], y_sb[c], SUB)
-        for c in range(TILES):
+        nc.vector.scalar_tensor_tensor(ga[2][:], ts_sa[0][:], us_high[:, 0:1], y_sb[2], MULT, SUB)
+        for c in range(3):
             nc.gpsimd.tensor_tensor(weights[c][:], ga[c][:], ts_all[:], MULT)
+        for c in range(2):
+            square(1, c, za[c][:], scratch("za_sq%d" % c))
+        for j in range(2):
+            square(1, 2 + j, ts_sa[j][:], scratch("za_sq%d" % j), scale=us_high[:, j:j + 1])
 
         b_op = operand("b", shared.tile([P, SLOTS, PACK], BF16, name="b_grouped", align_bytes=64, offset=16384))
         gather_operand(b_op, wb_planes, shared.tile([P, 2, SLOTS], BF16, name="b_pair", offset=1024))
-        sb = [bank(4 + c) for c in range(TILES)]
+        ga.append(scratch("wb3"))
+        nc.vector.scalar_tensor_tensor(ga[3][:], ts_sa[1][:], us_high[:, 1:2], y_sb[3], MULT, SUB)
+        nc.gpsimd.tensor_tensor(weights[3][:], ga[3][:], ts_all[:], MULT)
+        sb = [bank((6 + c) % 8) for c in range(TILES)]
         scores(sb[0], b_op, 0, 0, HALF, True, True)
         scores(sb[0], b_op, 0, HALF, SLOTS, True, True)
         for c in range(1, TILES):
             scores(sb[c], b_op, c, 0, SLOTS, True, True)
-        for c in range(TILES):
+        for c in range(3):
             square(2, c, ga[c][:], scratch_at("ga_sq%d" % c, 0))
+        square(0, 3, y_sb[3], scratch_at("y_sq3", 2048))
+        square(2, 3, ga[3][:], scratch_at("ga_sq3", 0))
         rest = keep.tile([P, 3, TILES], F32, name="rest")
         nc.gpsimd.tensor_tensor(rest[:, 0, :], squares[:, 0, :], squares[:, 1, :], SUB)
         nc.gpsimd.tensor_tensor(rest[:, 1, :], rest[:, 0, :], squares[:, 2, :], ADD)

@@ -9,6 +9,7 @@ PACK = 4
 TILES = R // P
 BLOCKS = SLOTS // P
 HALF = SLOTS // 2
+QUARTER = T // 4
 
 F32 = mybir.dt.float32
 BF16 = mybir.dt.bfloat16
@@ -20,6 +21,7 @@ MULT = mybir.AluOpType.mult
 ADD = mybir.AluOpType.add
 SUB = mybir.AluOpType.subtract
 COPY = mybir.ActivationFunctionType.Copy
+IDENTITY = mybir.ActivationFunctionType.Identity
 SQUARE = mybir.ActivationFunctionType.Square
 
 FLOPS = 2 * 2 * D * R * SLOTS
@@ -46,24 +48,23 @@ def tile_attend_gtrace_sq_kernel(tc, xT, wa, wb, us, ts, xx, y, offs, out):
         wa_planes = [keep.tile([P, T], F32, name="wa%d" % t) for t in range(PACK)]
         wb_planes = [keep.tile([P, T], F32, name="wb%d" % t) for t in range(PACK)]
         x_raw = keep.tile([P, PACK, R], F32, name="x_raw")
-        y_pair = keep.tile([P, 2, SLOTS], F32, name="y_pair")
-        y_sb = [y_pair[:, 0, :], y_pair[:, 1, :], scratch_at("y2", 16384)[:], scratch("y3")[:]]
+        y_early = keep.tile([P, 3, SLOTS], F32, name="y_early")
+        y_sb = [y_early[:, c, :] for c in range(3)] + [scratch("y_late")[:]]
         wa_v = wa.rearrange("(p t) w -> p t w", t=PACK)
         wb_v = wb.rearrange("(p t) w -> p t w", t=PACK)
         y_v = y.rearrange("(c p) i -> p c i", p=P)
 
-        ts_stage = keep.tile([1, T], F32, name="ts_stage")
+        ts_stage = keep.tile([P, QUARTER], F32, name="ts_stage")
         us_stage = keep.tile([2 * TILES, P], F32, name="us_stage")
-        nc.sync.dma_start(out=ts_stage[:], in_=ts[0:1, :])
+        nc.sync.dma_start(out=ts_stage[0:P:32, :], in_=ts[0:1, :].rearrange("o (q w) -> (o q) w", q=4))
         nc.sync.dma_start(out=wa_planes[0][:], in_=wa_v[:, 0, :])
         nc.sync.dma_start(offsets[:], offs)
-        nc.sync.dma_start(out=us_stage[0:TILES, :], in_=us.rearrange("(c p) o -> c (p o)", p=P))
-        nc.sync.dma_start(out=us_stage[TILES:2 * TILES, :], in_=xx.rearrange("(c p) o -> c (p o)", p=P))
+        nc.scalar.dma_start(out=us_stage[0:TILES, :], in_=us.rearrange("(c p) o -> c (p o)", p=P))
+        nc.scalar.dma_start(out=us_stage[TILES:2 * TILES, :], in_=xx.rearrange("(c p) o -> c (p o)", p=P))
         for t in range(1, PACK):
             nc.sync.dma_start(out=wa_planes[t][:], in_=wa_v[:, t, :])
         nc.sync.dma_start(out=x_raw[:], in_=xT.rearrange("(p t) r -> p t r", t=PACK))
-        nc.sync.dma_start(out=y_pair[:], in_=y_v[:, 0:2, :])
-        nc.sync.dma_start(out=y_sb[2], in_=y_v[:, 2, :])
+        nc.sync.dma_start(out=y_early[:], in_=y_v[:, 0:3, :])
         for t in range(PACK):
             nc.sync.dma_start(out=wb_planes[t][:], in_=wb_v[:, t, :])
         nc.sync.dma_start(out=y_sb[3], in_=y_v[:, 3, :])
@@ -75,20 +76,27 @@ def tile_attend_gtrace_sq_kernel(tc, xT, wa, wb, us, ts, xx, y, offs, out):
         nc.vector.memset(row_scales[:], 0.0)
         nc.vector.memset(ts_win[:], 0.0)
         nc.vector.memset(res_cols[:], 0.0)
+        ones = keep.tile([P, 1], F32, name="ones")
+        nc.vector.memset(ones[:], 1.0)
         make_identity(nc, ident[:])
-        nc.vector.tensor_copy(ts_win[0:1, :], ts_stage[:])
+        closing = bank(7)
+        nc.tensor.transpose(closing[:, HALF:HALF + P], ones[:].to_broadcast([P, P]), ident[:])
+        for q in range(4):
+            nc.vector.tensor_copy(ts_win[32 * q:32 * q + 1, q * QUARTER:(q + 1) * QUARTER], ts_stage[32 * q:32 * q + 1, :])
         nc.scalar.activation(row_scales[0:2 * TILES, :], us_stage[:], COPY)
 
         turned = bank(4)
         nc.tensor.transpose(turned[:, 0:P], row_scales[:], ident[:])
-        us_low = shared.tile([P, 2], F32, name="us_low", offset=1024)
-        nc.scalar.copy(out=us_low[:], in_=turned[:, 0:2])
-        us_high = keep.tile([P, 2], F32, name="us_high")
-        nc.scalar.copy(out=us_high[:], in_=turned[:, 2:TILES])
+        us_straight = shared.tile([P, 3], F32, name="us_straight", offset=1024)
+        nc.scalar.copy(out=us_straight[:], in_=turned[:, 0:3])
+        us_last = keep.tile([P, 1], F32, name="us_last")
+        nc.scalar.copy(out=us_last[:], in_=turned[:, 3:4])
         xx_cols = keep.tile([P, TILES], F32, name="xx_cols")
         nc.scalar.copy(out=xx_cols[:], in_=turned[:, TILES:2 * TILES])
         half_xx = keep.tile([P, TILES], F32, name="half_xx")
         nc.scalar.activation(half_xx[:], turned[:, TILES:2 * TILES], COPY, scale=0.5)
+        neg_half_xx = keep.tile([P, TILES], F32, name="neg_half_xx")
+        nc.scalar.activation(neg_half_xx[:], turned[:, TILES:2 * TILES], COPY, scale=-0.5)
         us_xx = keep.tile([P, TILES], F32, name="us_xx")
         for c in range(TILES):
             nc.scalar.activation(us_xx[:, c:c + 1], turned[:, c:c + 1], COPY, scale=xx_cols[:, c:c + 1])
@@ -101,10 +109,12 @@ def tile_attend_gtrace_sq_kernel(tc, xT, wa, wb, us, ts, xx, y, offs, out):
         turned = bank(5)
         for b in range(BLOCKS):
             nc.tensor.transpose(block(turned, b), block(ts_row, b), ident[:])
-        ts_cols = shared.tile([P, BLOCKS], F32, name="ts_cols", offset=22528)
-        nc.scalar.copy(out=ts_cols[:], in_=turned[:, 0:SLOTS:P])
         ts_scale = keep.tile([P, BLOCKS], F32, name="ts_scale")
-        nc.scalar.copy(out=ts_scale[:], in_=turned[:, 0:SLOTS:P])
+        for b in range(BLOCKS):
+            nc.scalar.activation(keep.tile([P, 4], F32, name="ts_parts%d" % b)[:], block(turned, b)[:, 0:P:32], COPY,
+                                 accum_out=ts_scale[:, b:b + 1])
+        ts_cols = shared.tile([P, BLOCKS], F32, name="ts_cols", offset=22528)
+        nc.scalar.copy(out=ts_cols[:], in_=ts_scale[:])
         turned = bank(6)
         for b in range(BLOCKS):
             nc.tensor.transpose(block(turned, b), ts_cols[:, b:b + 1].to_broadcast([P, P]), ident[:])
@@ -135,16 +145,15 @@ def tile_attend_gtrace_sq_kernel(tc, xT, wa, wb, us, ts, xx, y, offs, out):
             for c0 in (0, HALF):
                 quantize(op, c0, c0 + HALF, op[0][:, c0:c0 + HALF, :])
 
-        def scores(dst, w_op, c, c0, c1, start, stop):
-            rows = slice(c * P, (c + 1) * P)
+        def product(dst, stationary, s0, moving, m0, m1):
             nc.tensor.matmul_mx(
-                out=dst[:, c0:c1],
-                lhsT=x_op[1][:, rows].bitcast(FP8X4),
-                lhsT_scale=x_op[2][:, rows],
-                rhs=w_op[1][:, c0:c1].bitcast(FP8X4),
-                rhs_scale=w_op[2][:, c0:c1],
-                start=start,
-                stop=stop,
+                out=dst,
+                lhsT=stationary[1][:, s0:s0 + P].bitcast(FP8X4),
+                lhsT_scale=stationary[2][:, s0:s0 + P],
+                rhs=moving[1][:, m0:m1].bitcast(FP8X4),
+                rhs_scale=moving[2][:, m0:m1],
+                start=True,
+                stop=True,
             )
 
         x_op = operand("x", None)
@@ -163,69 +172,78 @@ def tile_attend_gtrace_sq_kernel(tc, xT, wa, wb, us, ts, xx, y, offs, out):
 
         squares = keep.tile([P, 3, TILES], F32, name="squares")
         acc = keep.tile([P, TILES], F32, name="acc")
+        rest = keep.tile([P, TILES], F32, name="rest")
+        partial = keep.tile([P, 2, TILES], F32, name="partial")
 
         def square(kind, c, src, unused, scale=1.0):
             nc.scalar.activation(unused[:], src, SQUARE, scale=scale, accum_out=squares[:, kind, c:c + 1])
 
+        def add_half_xx(dst, kind, c, before):
+            nc.scalar.activation(dst[:, c:c + 1], squares[:, kind, c:c + 1], IDENTITY, scale=half_xx[:, c:c + 1],
+                                 bias=before[:, c:c + 1])
+
         for c in range(3):
             square(0, c, y_sb[c], scratch_at("y_sq%d" % c, 11776 + 2048 * (c % 2)))
+        za = [scratch("za0"), scratch_at("za1", 16384), scratch("za2")]
+        for c in range(3):
+            sa = bank(c)
+            product(sa[:], x_op, c * P, a_op, 0, SLOTS)
+            nc.vector.scalar_tensor_tensor(za[c][:], sa[:], us_straight[:, c:c + 1], ts_all[:], MULT, MULT)
+        turned_scores = bank(3)
+        for b in range(BLOCKS):
+            product(block(turned_scores, b), a_op, b * P, x_op, 3 * P, R)
+        scaled = scratch("scaled")
+        for b in range(BLOCKS):
+            nc.scalar.activation(block(scaled, b), block(turned_scores, b), COPY, scale=ts_scale[:, b:b + 1])
+        ts_sa = bank(4)
+        for b in range(BLOCKS):
+            nc.tensor.transpose(block(ts_sa, b), block(scaled, b), ident[:])
         ga = [scratch("ga%d" % c) for c in range(3)]
         weights = [scratch("weights%d" % c) for c in range(TILES)]
-        za = [scratch("za%d" % c) for c in range(2)]
-        for c in range(2):
-            sa = bank(c)
-            scores(sa, a_op, c, 0, SLOTS, True, True)
-            nc.vector.scalar_tensor_tensor(za[c][:], sa[:], us_low[:, c:c + 1], ts_all[:], MULT, MULT)
-        turned_scores = [psum.tile([P, 2, HALF], F32, name="bank%d" % (2 + j)) for j in range(2)]
-        scaled = keep.tile([P, BLOCKS, HALF], F32, name="scaled")
-        for b in range(BLOCKS):
-            nc.tensor.matmul_mx(
-                out=turned_scores[b // 2][:, b % 2, :],
-                lhsT=block(a_op[1], b).bitcast(FP8X4),
-                lhsT_scale=block(a_op[2], b),
-                rhs=x_op[1][:, HALF:R].bitcast(FP8X4),
-                rhs_scale=x_op[2][:, HALF:R],
-                start=True,
-                stop=True,
-            )
-        for b in range(BLOCKS):
-            nc.scalar.activation(scaled[:, b, :], turned_scores[b // 2][:, b % 2, :], COPY, scale=ts_scale[:, b:b + 1])
-        ts_sa = [bank(4 + j) for j in range(2)]
-        for j in range(2):
-            for b in range(BLOCKS):
-                nc.tensor.transpose(block(ts_sa[j], b), scaled[:, b, j * P:(j + 1) * P], ident[:])
-        for c in range(2):
+        for c in range(3):
             nc.gpsimd.tensor_tensor(ga[c][:], za[c][:], y_sb[c], SUB)
-        nc.vector.scalar_tensor_tensor(ga[2][:], ts_sa[0][:], us_high[:, 0:1], y_sb[2], MULT, SUB)
         for c in range(3):
             nc.gpsimd.tensor_tensor(weights[c][:], ga[c][:], ts_all[:], MULT)
+        closing_weights = keep.tile([P, HALF + 1], F32, name="closing_weights")
+        nc.gpsimd.tensor_scalar(closing_weights[:, 0:HALF], weights[0][:, HALF:SLOTS], us_xx[:, 0:1], 0.0, MULT, ADD)
+        for c in range(3):
+            square(1, c, za[c][:], scratch("za_sq%d" % (c % 2)))
+        square(1, 3, ts_sa[:], scratch("za_sq1"), scale=us_last[:])
         for c in range(2):
-            square(1, c, za[c][:], scratch("za_sq%d" % c))
-        for j in range(2):
-            square(1, 2 + j, ts_sa[j][:], scratch("za_sq%d" % j), scale=us_high[:, j:j + 1])
+            square(2, c, ga[c][:], scratch("za_sq%d" % c))
 
         b_op = operand("b", shared.tile([P, SLOTS, PACK], BF16, name="b_grouped", align_bytes=64, offset=16384))
         gather_operand(b_op, wb_planes, shared.tile([P, 2, SLOTS], BF16, name="b_pair", offset=1024))
         ga.append(scratch("wb3"))
-        nc.vector.scalar_tensor_tensor(ga[3][:], ts_sa[1][:], us_high[:, 1:2], y_sb[3], MULT, SUB)
+        nc.vector.scalar_tensor_tensor(ga[3][:], ts_sa[:], us_last[:], y_sb[3], MULT, SUB)
         nc.gpsimd.tensor_tensor(weights[3][:], ga[3][:], ts_all[:], MULT)
-        sb = [bank((6 + c) % 8) for c in range(TILES)]
-        scores(sb[0], b_op, 0, 0, HALF, True, True)
-        scores(sb[0], b_op, 0, HALF, SLOTS, True, True)
-        for c in range(1, TILES):
-            scores(sb[c], b_op, c, 0, SLOTS, True, True)
-        for c in range(3):
-            square(2, c, ga[c][:], scratch_at("ga_sq%d" % c, 0))
-        square(0, 3, y_sb[3], scratch_at("y_sq3", 2048))
-        square(2, 3, ga[3][:], scratch_at("ga_sq3", 0))
-        rest = keep.tile([P, 3, TILES], F32, name="rest")
-        nc.gpsimd.tensor_tensor(rest[:, 0, :], squares[:, 0, :], squares[:, 1, :], SUB)
-        nc.gpsimd.tensor_tensor(rest[:, 1, :], rest[:, 0, :], squares[:, 2, :], ADD)
-        nc.gpsimd.tensor_tensor(rest[:, 2, :], rest[:, 1, :], half_xx[:], MULT)
+        sb = [bank(c) for c in range(3)] + [bank(5)]
+        product(sb[0][:, 0:HALF], x_op, 0, b_op, 0, HALF)
+        product(sb[1][:, 0:HALF], x_op, P, b_op, 0, HALF)
+        product(sb[1][:, HALF:SLOTS], x_op, P, b_op, HALF, SLOTS)
+        for c in (2, 3):
+            product(sb[c][:], x_op, c * P, b_op, 0, SLOTS)
+        product(closing[:, 0:HALF], x_op, 0, b_op, HALF, SLOTS)
+
+        square(2, 2, ga[2][:], scratch_at("ga_sq2", 0))
         for c in range(TILES):
-            nc.vector.scalar_tensor_tensor(scratch("last%d" % c)[:], sb[c][:], us_xx[:, c:c + 1], weights[c][:],
-                                           MULT, MULT, accum_out=acc[:, c:c + 1])
-        nc.vector.tensor_tensor(res_cols[:, 0:P:32], acc[:], rest[:, 2, :], ADD)
+            nc.scalar.activation(partial[:, 0, c:c + 1], squares[:, 1, c:c + 1], COPY, scale=neg_half_xx[:, c:c + 1])
+        for c in range(3):
+            add_half_xx(partial[:, 1, :], 0, c, partial[:, 0, :])
+            add_half_xx(rest, 2, c, partial[:, 1, :])
+        square(0, 3, y_sb[3], scratch_at("y_sq3", 2048))
+        add_half_xx(partial[:, 1, :], 0, 3, partial[:, 0, :])
+        square(2, 3, ga[3][:], scratch_at("ga_sq3", 0))
+        add_half_xx(rest, 2, 3, partial[:, 1, :])
+
+        for c in range(TILES):
+            width = HALF if c == 0 else SLOTS
+            nc.vector.scalar_tensor_tensor(scratch("last%d" % c)[:, 0:width], sb[c][:, 0:width], us_xx[:, c:c + 1],
+                                           weights[c][:, 0:width], MULT, MULT, accum_out=acc[:, c:c + 1])
+            total = closing_weights[:, HALF:HALF + 1] if c == 0 else res_cols[:, 32 * c:32 * c + 1]
+            nc.scalar.activation(total, acc[:, c:c + 1], IDENTITY, bias=rest[:, c:c + 1])
+        nc.vector.scalar_tensor_tensor(scratch("last4")[:, 0:HALF + 1], closing[:, 0:HALF + 1], 1.0, closing_weights[:],
+                                       MULT, MULT, accum_out=res_cols[:, 0:1])
         res_rows = keep.tile([P, P], F32, name="res_rows", align_bytes=64)
         nc.vector.transpose(res_rows[:], res_cols[:])
         nc.sync.dma_start(

@@ -18,7 +18,6 @@ U16 = mybir.dt.uint16
 U8 = mybir.dt.uint8
 FP8X4 = mybir.dt.float8_e4m3fn_x4
 MULT = mybir.AluOpType.mult
-ADD = mybir.AluOpType.add
 SUB = mybir.AluOpType.subtract
 COPY = mybir.ActivationFunctionType.Copy
 IDENTITY = mybir.ActivationFunctionType.Identity
@@ -45,8 +44,10 @@ def tile_attend_gtrace_sq_kernel(tc, xT, wa, wb, us, ts, xx, y, offs, out):
             return shared.tile([P, SLOTS], F32, name=name, offset=offset)
 
         offsets = keep.tile([P, SLOTS // 16], U16, name="offsets")
-        wa_planes = [keep.tile([P, T], F32, name="wa%d" % t) for t in range(PACK)]
-        wb_planes = [keep.tile([P, T], F32, name="wb%d" % t) for t in range(PACK)]
+        wa_pairs = [keep.tile([P, 2, T], F32, name="wa_pair%d" % n) for n in range(2)]
+        wa_planes = [wa_pairs[t // 2][:, t % 2, :] for t in range(PACK)]
+        wb_pair = keep.tile([P, 2, T], F32, name="wb_pair")
+        wb_planes = [wb_pair[:, t, :] for t in range(2)] + [keep.tile([P, T], F32, name="wb%d" % t)[:] for t in (2, 3)]
         x_raw = keep.tile([P, PACK, R], F32, name="x_raw")
         y_early = keep.tile([P, 3, SLOTS], F32, name="y_early")
         y_sb = [y_early[:, c, :] for c in range(3)] + [scratch("y_late")[:]]
@@ -57,16 +58,16 @@ def tile_attend_gtrace_sq_kernel(tc, xT, wa, wb, us, ts, xx, y, offs, out):
         ts_stage = keep.tile([P, QUARTER], F32, name="ts_stage")
         us_stage = keep.tile([2 * TILES, P], F32, name="us_stage")
         nc.sync.dma_start(out=ts_stage[0:P:32, :], in_=ts[0:1, :].rearrange("o (q w) -> (o q) w", q=4))
-        nc.sync.dma_start(out=wa_planes[0][:], in_=wa_v[:, 0, :])
+        nc.sync.dma_start(out=wa_pairs[0][:], in_=wa_v[:, 0:2, :])
         nc.sync.dma_start(offsets[:], offs)
         nc.scalar.dma_start(out=us_stage[0:TILES, :], in_=us.rearrange("(c p) o -> c (p o)", p=P))
         nc.scalar.dma_start(out=us_stage[TILES:2 * TILES, :], in_=xx.rearrange("(c p) o -> c (p o)", p=P))
-        for t in range(1, PACK):
-            nc.sync.dma_start(out=wa_planes[t][:], in_=wa_v[:, t, :])
+        nc.sync.dma_start(out=wa_pairs[1][:], in_=wa_v[:, 2:4, :])
         nc.sync.dma_start(out=x_raw[:], in_=xT.rearrange("(p t) r -> p t r", t=PACK))
         nc.sync.dma_start(out=y_early[:], in_=y_v[:, 0:3, :])
-        for t in range(PACK):
-            nc.sync.dma_start(out=wb_planes[t][:], in_=wb_v[:, t, :])
+        nc.sync.dma_start(out=wb_pair[:], in_=wb_v[:, 0:2, :])
+        for t in (2, 3):
+            nc.sync.dma_start(out=wb_planes[t], in_=wb_v[:, t, :])
         nc.sync.dma_start(out=y_sb[3], in_=y_v[:, 3, :])
 
         ts_win = keep.tile([P, T], F32, name="ts_win")
@@ -91,12 +92,15 @@ def tile_attend_gtrace_sq_kernel(tc, xT, wa, wb, us, ts, xx, y, offs, out):
         nc.scalar.copy(out=us_straight[:], in_=turned[:, 0:3])
         us_last = keep.tile([P, 1], F32, name="us_last")
         nc.scalar.copy(out=us_last[:], in_=turned[:, 3:4])
+        us_first = keep.tile([P, 1], F32, name="us_first")
+        nc.scalar.copy(out=us_first[:], in_=turned[:, 0:1])
         xx_cols = keep.tile([P, TILES], F32, name="xx_cols")
         nc.scalar.copy(out=xx_cols[:], in_=turned[:, TILES:2 * TILES])
-        half_xx = keep.tile([P, TILES], F32, name="half_xx")
-        nc.scalar.activation(half_xx[:], turned[:, TILES:2 * TILES], COPY, scale=0.5)
-        neg_half_xx = keep.tile([P, TILES], F32, name="neg_half_xx")
-        nc.scalar.activation(neg_half_xx[:], turned[:, TILES:2 * TILES], COPY, scale=-0.5)
+        half_xx = keep.tile([P, 2], F32, name="half_xx")
+        nc.scalar.activation(half_xx[:], turned[:, TILES:TILES + 2], COPY, scale=0.5)
+        neg_xx = keep.tile([P, TILES], F32, name="neg_xx")
+        nc.scalar.activation(neg_xx[:, 0:2], turned[:, TILES:TILES + 2], COPY, scale=-0.5)
+        nc.scalar.activation(neg_xx[:, 2:4], turned[:, TILES + 2:2 * TILES], COPY, scale=-1.0)
         us_xx = keep.tile([P, TILES], F32, name="us_xx")
         for c in range(TILES):
             nc.scalar.activation(us_xx[:, c:c + 1], turned[:, c:c + 1], COPY, scale=xx_cols[:, c:c + 1])
@@ -120,6 +124,9 @@ def tile_attend_gtrace_sq_kernel(tc, xT, wa, wb, us, ts, xx, y, offs, out):
             nc.tensor.transpose(block(turned, b), ts_cols[:, b:b + 1].to_broadcast([P, P]), ident[:])
         ts_all = scratch("ts_all")
         nc.scalar.copy(out=ts_all[:], in_=turned[:])
+        ts_first = scratch("ts_first")
+        nc.scalar.copy(out=ts_first[:, 0:HALF], in_=turned[:, 0:HALF])
+        nc.scalar.activation(ts_first[:, HALF:SLOTS], turned[:, HALF:SLOTS], COPY, scale=us_xx[:, 0:1])
 
         def operand(name, grouped):
             codes = keep.tile([P, SLOTS], U32, name=name + "_codes", align_bytes=64)
@@ -136,30 +143,30 @@ def tile_attend_gtrace_sq_kernel(tc, xT, wa, wb, us, ts, xx, y, offs, out):
 
         def gather_operand(op, planes, pair):
             for t in range(2):
-                nc.vector.tensor_copy(pair[:, t, :], planes[t][:].indirect(offsets[:]))
+                nc.vector.tensor_copy(pair[:, t, :], planes[t].indirect(offsets[:]))
             nc.scalar.copy(out=op[0][:, :, 0:2], in_=pair[:].rearrange("p t s -> p s t"))
-            nc.vector.tensor_copy(op[0][:, :, 2], planes[2][:].indirect(offsets[:]))
+            nc.vector.tensor_copy(op[0][:, :, 2], planes[2].indirect(offsets[:]))
             for c0 in (0, HALF):
                 nc.vector.tensor_copy(op[0][:, c0:c0 + HALF, 3],
-                                      planes[3][:].indirect(offsets[:, c0 // 16:(c0 + HALF) // 16]))
+                                      planes[3].indirect(offsets[:, c0 // 16:(c0 + HALF) // 16]))
             for c0 in (0, HALF):
                 quantize(op, c0, c0 + HALF, op[0][:, c0:c0 + HALF, :])
 
-        def product(dst, stationary, s0, moving, m0, m1):
+        def product(dst, stationary, s0, moving, m0, m1, start=True, stop=True):
             nc.tensor.matmul_mx(
                 out=dst,
                 lhsT=stationary[1][:, s0:s0 + P].bitcast(FP8X4),
                 lhsT_scale=stationary[2][:, s0:s0 + P],
                 rhs=moving[1][:, m0:m1].bitcast(FP8X4),
                 rhs_scale=moving[2][:, m0:m1],
-                start=True,
-                stop=True,
+                start=start,
+                stop=stop,
             )
 
         x_op = operand("x", None)
         a_op = operand("a", keep.tile([P, SLOTS, PACK], BF16, name="a_grouped", align_bytes=64))
 
-        gather_operand(a_op, wa_planes, shared.tile([P, 2, SLOTS], BF16, name="a_pair", offset=13312))
+        gather_operand(a_op, wa_planes, shared.tile([P, 2, SLOTS], F32, name="a_pair", offset=11776))
         x_grouped = [shared.tile([P, P, PACK], BF16, name="x_first", align_bytes=64, offset=13312),
                      shared.tile([P, R - P, PACK], BF16, name="x_rest", align_bytes=64, offset=20480)]
         x_tiles = [x_grouped[0][:]] + [x_grouped[1][:, c * P:(c + 1) * P, :] for c in range(TILES - 1)]
@@ -185,10 +192,16 @@ def tile_attend_gtrace_sq_kernel(tc, xT, wa, wb, us, ts, xx, y, offs, out):
         for c in range(3):
             square(0, c, y_sb[c], scratch_at("y_sq%d" % c, 11776 + 2048 * (c % 2)))
         za = [scratch("za0"), scratch_at("za1", 16384), scratch("za2")]
+        ga = [scratch("ga%d" % c) for c in range(3)]
         for c in range(3):
             sa = bank(c)
             product(sa[:], x_op, c * P, a_op, 0, SLOTS)
-            nc.vector.scalar_tensor_tensor(za[c][:], sa[:], us_straight[:, c:c + 1], ts_all[:], MULT, MULT)
+            if c == 0:
+                nc.vector.tensor_tensor(za[c][:], sa[:], ts_all[:], MULT)
+            else:
+                nc.vector.scalar_tensor_tensor(za[c][:], sa[:], us_straight[:, c:c + 1], ts_all[:], MULT, MULT)
+            if c == 1:
+                nc.vector.scalar_tensor_tensor(ga[0][:], za[0][:], us_straight[:, 0:1], y_sb[0], MULT, SUB)
         turned_scores = bank(3)
         for b in range(BLOCKS):
             product(block(turned_scores, b), a_op, b * P, x_op, 3 * P, R)
@@ -198,43 +211,42 @@ def tile_attend_gtrace_sq_kernel(tc, xT, wa, wb, us, ts, xx, y, offs, out):
         ts_sa = bank(4)
         for b in range(BLOCKS):
             nc.tensor.transpose(block(ts_sa, b), block(scaled, b), ident[:])
-        ga = [scratch("ga%d" % c) for c in range(3)]
-        weights = [scratch("weights%d" % c) for c in range(TILES)]
-        for c in range(3):
+        weights = [keep.tile([P, SLOTS + 1], F32, name="weights0")] + [scratch("weights%d" % c) for c in range(1, TILES)]
+        for c in (1, 2):
             nc.gpsimd.tensor_tensor(ga[c][:], za[c][:], y_sb[c], SUB)
         for c in range(3):
-            nc.gpsimd.tensor_tensor(weights[c][:], ga[c][:], ts_all[:], MULT)
-        closing_weights = keep.tile([P, HALF + 1], F32, name="closing_weights")
-        nc.gpsimd.tensor_scalar(closing_weights[:, 0:HALF], weights[0][:, HALF:SLOTS], us_xx[:, 0:1], 0.0, MULT, ADD)
-        for c in range(3):
+            nc.gpsimd.tensor_tensor(weights[c][:, 0:SLOTS], ga[c][:], (ts_all if c else ts_first)[:], MULT)
+        closing_weights = weights[0][:, HALF:SLOTS + 1]
+        square(1, 0, za[0][:], scratch("za_sq0"), scale=us_first[:])
+        for c in (1, 2):
             square(1, c, za[c][:], scratch("za_sq%d" % (c % 2)))
         square(1, 3, ts_sa[:], scratch("za_sq1"), scale=us_last[:])
-        for c in range(2):
-            square(2, c, ga[c][:], scratch("za_sq%d" % c))
 
+        sb = [bank(c) for c in range(3)] + [bank(5)]
+        for c in (2, 3):
+            product(sb[c][:], x_op, c * P, a_op, 0, SLOTS, stop=False)
         b_op = operand("b", shared.tile([P, SLOTS, PACK], BF16, name="b_grouped", align_bytes=64, offset=16384))
-        gather_operand(b_op, wb_planes, shared.tile([P, 2, SLOTS], BF16, name="b_pair", offset=1024))
+        gather_operand(b_op, wb_planes, shared.tile([P, 2, SLOTS], F32, name="b_pair", offset=0))
         ga.append(scratch("wb3"))
         nc.vector.scalar_tensor_tensor(ga[3][:], ts_sa[:], us_last[:], y_sb[3], MULT, SUB)
         nc.gpsimd.tensor_tensor(weights[3][:], ga[3][:], ts_all[:], MULT)
-        sb = [bank(c) for c in range(3)] + [bank(5)]
         product(sb[0][:, 0:HALF], x_op, 0, b_op, 0, HALF)
         product(sb[1][:, 0:HALF], x_op, P, b_op, 0, HALF)
         product(sb[1][:, HALF:SLOTS], x_op, P, b_op, HALF, SLOTS)
         for c in (2, 3):
-            product(sb[c][:], x_op, c * P, b_op, 0, SLOTS)
+            product(sb[c][:], x_op, c * P, b_op, 0, SLOTS, start=False)
         product(closing[:, 0:HALF], x_op, 0, b_op, HALF, SLOTS)
 
-        square(2, 2, ga[2][:], scratch_at("ga_sq2", 0))
         for c in range(TILES):
-            nc.scalar.activation(partial[:, 0, c:c + 1], squares[:, 1, c:c + 1], COPY, scale=neg_half_xx[:, c:c + 1])
-        for c in range(3):
+            nc.scalar.activation(partial[:, 0, c:c + 1], squares[:, 1, c:c + 1], COPY, scale=neg_xx[:, c:c + 1])
+        for c in range(2):
+            square(2, c, ga[c][:], scratch_at("ga_sq%d" % c, 2048 * c))
             add_half_xx(partial[:, 1, :], 0, c, partial[:, 0, :])
             add_half_xx(rest, 2, c, partial[:, 1, :])
         square(0, 3, y_sb[3], scratch_at("y_sq3", 2048))
-        add_half_xx(partial[:, 1, :], 0, 3, partial[:, 0, :])
-        square(2, 3, ga[3][:], scratch_at("ga_sq3", 0))
-        add_half_xx(rest, 2, 3, partial[:, 1, :])
+        for c in (2, 3):
+            nc.scalar.activation(rest[:, c:c + 1], squares[:, 0, c:c + 1], IDENTITY, scale=xx_cols[:, c:c + 1],
+                                 bias=partial[:, 0, c:c + 1])
 
         for c in range(TILES):
             width = HALF if c == 0 else SLOTS
@@ -242,7 +254,7 @@ def tile_attend_gtrace_sq_kernel(tc, xT, wa, wb, us, ts, xx, y, offs, out):
                                            weights[c][:, 0:width], MULT, MULT, accum_out=acc[:, c:c + 1])
             total = closing_weights[:, HALF:HALF + 1] if c == 0 else res_cols[:, 32 * c:32 * c + 1]
             nc.scalar.activation(total, acc[:, c:c + 1], IDENTITY, bias=rest[:, c:c + 1])
-        nc.vector.scalar_tensor_tensor(scratch("last4")[:, 0:HALF + 1], closing[:, 0:HALF + 1], 1.0, closing_weights[:],
+        nc.vector.scalar_tensor_tensor(scratch("last4")[:, 0:HALF + 1], closing[:, 0:HALF + 1], 1.0, closing_weights,
                                        MULT, MULT, accum_out=res_cols[:, 0:1])
         res_rows = keep.tile([P, P], F32, name="res_rows", align_bytes=64)
         nc.vector.transpose(res_rows[:], res_cols[:])

@@ -57,9 +57,9 @@ def tile_attend_gtrace_sq_kernel(tc, xT, wa, wb, us, ts, xx, y, offs, out):
 
         ts_stage = keep.tile([P, QUARTER], F32, name="ts_stage")
         us_stage = keep.tile([2 * TILES, P], F32, name="us_stage")
-        nc.sync.dma_start(out=ts_stage[0:P:32, :], in_=ts[0:1, :].rearrange("o (q w) -> (o q) w", q=4))
         nc.sync.dma_start(out=wa_pairs[0][:], in_=wa_v[:, 0:2, :])
         nc.sync.dma_start(offsets[:], offs)
+        nc.scalar.dma_start(out=ts_stage[0:P:32, :], in_=ts[0:1, :].rearrange("o (q w) -> (o q) w", q=4))
         nc.scalar.dma_start(out=us_stage[0:TILES, :], in_=us.rearrange("(c p) o -> c (p o)", p=P))
         nc.scalar.dma_start(out=us_stage[TILES:2 * TILES, :], in_=xx.rearrange("(c p) o -> c (p o)", p=P))
         nc.sync.dma_start(out=wa_pairs[1][:], in_=wa_v[:, 2:4, :])

@@ -10,6 +10,8 @@ TILES = R // P
 BLOCKS = SLOTS // P
 HALF = SLOTS // 2
 QUARTER = T // 4
+LEAD = 16
+ROW = 4 * SLOTS
 
 F32 = mybir.dt.float32
 BF16 = mybir.dt.bfloat16
@@ -17,8 +19,10 @@ U32 = mybir.dt.uint32
 U16 = mybir.dt.uint16
 U8 = mybir.dt.uint8
 FP8X4 = mybir.dt.float8_e4m3fn_x4
+ADD = mybir.AluOpType.add
 MULT = mybir.AluOpType.mult
 SUB = mybir.AluOpType.subtract
+AXIS_X = mybir.AxisListType.X
 COPY = mybir.ActivationFunctionType.Copy
 IDENTITY = mybir.ActivationFunctionType.Identity
 SQUARE = mybir.ActivationFunctionType.Square
@@ -33,6 +37,7 @@ def tile_attend_gtrace_sq_kernel(tc, xT, wa, wb, us, ts, xx, y, offs, out):
         keep = ctx.enter_context(tc.tile_pool(name="keep", bufs=1))
         shared = ctx.enter_context(tc.tile_pool(name="shared", bufs=1))
         psum = ctx.enter_context(tc.psum_pool(name="psum", bufs=1))
+        psum_pair = ctx.enter_context(tc.psum_pool(name="psum_pair", bufs=1))
 
         def bank(n):
             return psum.tile([P, SLOTS], F32, name="bank%d" % n)
@@ -40,12 +45,16 @@ def tile_attend_gtrace_sq_kernel(tc, xT, wa, wb, us, ts, xx, y, offs, out):
         def scratch(name):
             return keep.tile([P, SLOTS], F32, name=name)
 
-        def scratch_at(name, offset):
-            return shared.tile([P, SLOTS], F32, name=name, offset=offset)
+        def placed(name, shape, dtype, offset):
+            return shared.tile(shape, dtype, name=name, align_bytes=64, offset=offset)
+
+        def block(ap, b):
+            return ap[:, b * P:(b + 1) * P]
 
         offsets = keep.tile([P, SLOTS // 16], U16, name="offsets")
-        wa_pairs = [keep.tile([P, 2, T], F32, name="wa_pair%d" % n) for n in range(2)]
-        wa_planes = [wa_pairs[t // 2][:, t % 2, :] for t in range(PACK)]
+        first, second = offsets[:, 0:HALF // 16], offsets[:, HALF // 16:SLOTS // 16]
+        wa_pairs = [keep.tile([P, 2, T], F32, name="wa_pair")]
+        wa_planes = [wa_pairs[0][:, t, :] for t in range(2)] + [keep.tile([P, T], F32, name="wa%d" % t)[:] for t in (2, 3)]
         wb_pair = keep.tile([P, 2, T], F32, name="wb_pair")
         wb_planes = [wb_pair[:, t, :] for t in range(2)] + [keep.tile([P, T], F32, name="wb%d" % t)[:] for t in (2, 3)]
         x_raw = keep.tile([P, PACK, R], F32, name="x_raw")
@@ -55,14 +64,15 @@ def tile_attend_gtrace_sq_kernel(tc, xT, wa, wb, us, ts, xx, y, offs, out):
         wb_v = wb.rearrange("(p t) w -> p t w", t=PACK)
         y_v = y.rearrange("(c p) i -> p c i", p=P)
 
-        ts_stage = keep.tile([P, QUARTER], F32, name="ts_stage")
-        us_stage = keep.tile([2 * TILES, P], F32, name="us_stage")
+        ts_stage = placed("ts_stage", [P, QUARTER], F32, 2752)
+        us_stage = placed("us_stage", [2 * TILES, P], F32, 8 * ROW - 256)
         nc.sync.dma_start(out=wa_pairs[0][:], in_=wa_v[:, 0:2, :])
         nc.sync.dma_start(offsets[:], offs)
         nc.scalar.dma_start(out=ts_stage[0:P:32, :], in_=ts[0:1, :].rearrange("o (q w) -> (o q) w", q=4))
         nc.scalar.dma_start(out=us_stage[0:TILES, :], in_=us.rearrange("(c p) o -> c (p o)", p=P))
         nc.scalar.dma_start(out=us_stage[TILES:2 * TILES, :], in_=xx.rearrange("(c p) o -> c (p o)", p=P))
-        nc.sync.dma_start(out=wa_pairs[1][:], in_=wa_v[:, 2:4, :])
+        for t in (2, 3):
+            nc.sync.dma_start(out=wa_planes[t], in_=wa_v[:, t, :])
         nc.sync.dma_start(out=x_raw[:], in_=xT.rearrange("(p t) r -> p t r", t=PACK))
         nc.sync.dma_start(out=y_early[:], in_=y_v[:, 0:3, :])
         nc.sync.dma_start(out=wb_pair[:], in_=wb_v[:, 0:2, :])
@@ -74,188 +84,208 @@ def tile_attend_gtrace_sq_kernel(tc, xT, wa, wb, us, ts, xx, y, offs, out):
         row_scales = keep.tile([P, P], F32, name="row_scales")
         res_cols = keep.tile([P, P], F32, name="res_cols", align_bytes=64)
         ident = keep.tile([P, P], F32, name="ident")
+        ones = keep.tile([P, 1], F32, name="ones")
         nc.vector.memset(row_scales[:], 0.0)
         nc.vector.memset(ts_win[:], 0.0)
         nc.vector.memset(res_cols[:], 0.0)
-        ones = keep.tile([P, 1], F32, name="ones")
         nc.vector.memset(ones[:], 1.0)
         make_identity(nc, ident[:])
         closing = bank(7)
-        nc.tensor.transpose(closing[:, HALF:HALF + P], ones[:].to_broadcast([P, P]), ident[:])
+        nc.tensor.transpose(closing[:, 0:P], ones[:].to_broadcast([P, P]), ident[:])
         for q in range(4):
             nc.vector.tensor_copy(ts_win[32 * q:32 * q + 1, q * QUARTER:(q + 1) * QUARTER], ts_stage[32 * q:32 * q + 1, :])
         nc.scalar.activation(row_scales[0:2 * TILES, :], us_stage[:], COPY)
 
-        turned = bank(4)
+        turned = scale_cols = psum_pair.tile([P, 2 * SLOTS], F32, name="scale_cols", offset=0)
         nc.tensor.transpose(turned[:, 0:P], row_scales[:], ident[:])
-        us_straight = shared.tile([P, 3], F32, name="us_straight", offset=1024)
-        nc.scalar.copy(out=us_straight[:], in_=turned[:, 0:3])
-        us_last = keep.tile([P, 1], F32, name="us_last")
-        nc.scalar.copy(out=us_last[:], in_=turned[:, 3:4])
-        us_first = keep.tile([P, 1], F32, name="us_first")
-        nc.scalar.copy(out=us_first[:], in_=turned[:, 0:1])
+        us_cols = placed("us_cols", [P, 32], F32, 5 * ROW - 128)
+        nc.scalar.copy(out=us_cols[:, 0:TILES], in_=turned[:, 0:TILES])
         xx_cols = keep.tile([P, TILES], F32, name="xx_cols")
         nc.scalar.copy(out=xx_cols[:], in_=turned[:, TILES:2 * TILES])
-        half_xx = keep.tile([P, 2], F32, name="half_xx")
-        nc.scalar.activation(half_xx[:], turned[:, TILES:TILES + 2], COPY, scale=0.5)
-        neg_xx = keep.tile([P, TILES], F32, name="neg_xx")
-        nc.scalar.activation(neg_xx[:, 0:2], turned[:, TILES:TILES + 2], COPY, scale=-0.5)
-        nc.scalar.activation(neg_xx[:, 2:4], turned[:, TILES + 2:2 * TILES], COPY, scale=-1.0)
+        us_last = keep.tile([P, 1], F32, name="us_last")
+        nc.scalar.copy(out=us_last[:], in_=turned[:, TILES - 1:TILES])
         us_xx = keep.tile([P, TILES], F32, name="us_xx")
         for c in range(TILES):
             nc.scalar.activation(us_xx[:, c:c + 1], turned[:, c:c + 1], COPY, scale=xx_cols[:, c:c + 1])
 
-        def block(ap, b):
-            return ap[:, b * P:(b + 1) * P]
-
-        ts_row = scratch("ts_row")
-        nc.vector.tensor_copy(ts_row[:], ts_win[:].indirect(offsets[:]))
-        turned = bank(5)
-        for b in range(BLOCKS):
-            nc.tensor.transpose(block(turned, b), block(ts_row, b), ident[:])
-        ts_scale = keep.tile([P, BLOCKS], F32, name="ts_scale")
-        for b in range(BLOCKS):
-            nc.scalar.activation(keep.tile([P, 4], F32, name="ts_parts%d" % b)[:], block(turned, b)[:, 0:P:32], COPY,
-                                 accum_out=ts_scale[:, b:b + 1])
-        ts_cols = shared.tile([P, BLOCKS], F32, name="ts_cols", offset=22528)
-        nc.scalar.copy(out=ts_cols[:], in_=ts_scale[:])
-        turned = bank(6)
-        for b in range(BLOCKS):
-            nc.tensor.transpose(block(turned, b), ts_cols[:, b:b + 1].to_broadcast([P, P]), ident[:])
-        ts_all = scratch("ts_all")
-        nc.scalar.copy(out=ts_all[:], in_=turned[:])
-        ts_first = scratch("ts_first")
-        nc.scalar.copy(out=ts_first[:, 0:HALF], in_=turned[:, 0:HALF])
-        nc.scalar.activation(ts_first[:, HALF:SLOTS], turned[:, HALF:SLOTS], COPY, scale=us_xx[:, 0:1])
-
-        def operand(name, grouped):
+        def operand(name):
             codes = keep.tile([P, SLOTS], U32, name=name + "_codes", align_bytes=64)
             scales = keep.tile([P, SLOTS], U8, name=name + "_scales", align_bytes=64)
-            return grouped, codes, scales
+            return codes, scales
 
         def quantize(op, c0, c1, grouped):
-            codes, scales = op[1:]
             nc.vector.quantize_mx(
-                out=codes[:, c0:c1].bitcast(FP8X4),
-                scales=scales[:, c0:c1],
+                out=op[0][:, c0:c1].bitcast(FP8X4),
+                scales=op[1][:, c0:c1],
                 in_=grouped.rearrange("p w t -> p (w t)"),
             )
 
-        def gather_operand(op, planes, pair):
-            for t in range(2):
-                nc.vector.tensor_copy(pair[:, t, :], planes[t].indirect(offsets[:]))
-            nc.scalar.copy(out=op[0][:, :, 0:2], in_=pair[:].rearrange("p t s -> p s t"))
-            nc.vector.tensor_copy(op[0][:, :, 2], planes[2].indirect(offsets[:]))
-            for c0 in (0, HALF):
-                nc.vector.tensor_copy(op[0][:, c0:c0 + HALF, 3],
-                                      planes[3].indirect(offsets[:, c0 // 16:(c0 + HALF) // 16]))
-            for c0 in (0, HALF):
-                quantize(op, c0, c0 + HALF, op[0][:, c0:c0 + HALF, :])
-
-        def product(dst, stationary, s0, moving, m0, m1, start=True, stop=True):
+        def product(dst, c, moving, m0, m1, start=True, stop=True):
             nc.tensor.matmul_mx(
                 out=dst,
-                lhsT=stationary[1][:, s0:s0 + P].bitcast(FP8X4),
-                lhsT_scale=stationary[2][:, s0:s0 + P],
-                rhs=moving[1][:, m0:m1].bitcast(FP8X4),
-                rhs_scale=moving[2][:, m0:m1],
+                lhsT=block(x_op[0], c).bitcast(FP8X4),
+                lhsT_scale=block(x_op[1], c),
+                rhs=moving[0][:, m0:m1].bitcast(FP8X4),
+                rhs_scale=moving[1][:, m0:m1],
                 start=start,
                 stop=stop,
             )
 
-        x_op = operand("x", None)
-        a_op = operand("a", keep.tile([P, SLOTS, PACK], BF16, name="a_grouped", align_bytes=64))
+        def pair_up(grouped, stage):
+            nc.scalar.copy(out=grouped, in_=stage.rearrange("p t s -> p s t"))
 
-        gather_operand(a_op, wa_planes, shared.tile([P, 2, SLOTS], F32, name="a_pair", offset=11776))
-        x_grouped = [shared.tile([P, P, PACK], BF16, name="x_first", align_bytes=64, offset=13312),
-                     shared.tile([P, R - P, PACK], BF16, name="x_rest", align_bytes=64, offset=20480)]
-        x_tiles = [x_grouped[0][:]] + [x_grouped[1][:, c * P:(c + 1) * P, :] for c in range(TILES - 1)]
-        for c in range(TILES):
-            copy = nc.vector.tensor_copy if c < 1 else nc.scalar.copy
-            copy(out=x_tiles[c].rearrange("p (c i) t -> p c t i", i=4),
+        def second_plane(grouped, low, plane):
+            for c0, half in ((0, first), (HALF, second)):
+                nc.vector.tensor_copy(low[:, 1, c0:c0 + HALF], plane.indirect(half))
+                pair_up(grouped[:, c0:c0 + HALF, 0:2], low[:, :, c0:c0 + HALF])
+
+        x_op, a_op = operand("x"), operand("a")
+
+        a_grouped = placed("a_grouped", [P, SLOTS, PACK], BF16, 8 * ROW)
+        a_low = placed("a_low", [P, 2, SLOTS], F32, 2816)[:]
+        a_high = placed("a_high", [P, 2, HALF], F32, 768)[:]
+        ts_row = placed("ts_row", [P, SLOTS], F32, 9 * ROW)
+        nc.vector.tensor_copy(ts_row[:], ts_win[:].indirect(offsets[:]))
+        turned = bank(2)
+        for b in range(BLOCKS):
+            nc.tensor.transpose(block(turned, b), block(ts_row, b), ident[:])
+        nc.vector.tensor_copy(a_low[:, 0, :], wa_planes[0].indirect(offsets[:]))
+        ts_cols = keep.tile([P, BLOCKS], F32, name="ts_cols")
+        nc.vector.tensor_reduce(ts_cols[:], turned[:].rearrange("p (b q j) -> p b q j", b=BLOCKS, q=4)[:, :, :, 0], AXIS_X, ADD)
+        turned = bank(3)
+        for b in range(BLOCKS):
+            nc.tensor.transpose(block(turned, b), ts_cols[:, b:b + 1].to_broadcast([P, P]), ident[:])
+        ts_all = placed("ts_all", [P, SLOTS], F32, 7 * ROW)
+        nc.scalar.copy(out=ts_all[:], in_=turned[:])
+        ts_first = scratch("ts_first")
+        nc.gpsimd.tensor_scalar(ts_first[:], ts_all[:], us_xx[:, 0:1], 0.0, MULT, ADD)
+        second_plane(a_grouped, a_low, wa_planes[1])
+        for t in (2, 3):
+            nc.vector.tensor_copy(a_high[:, t - 2, :], wa_planes[t].indirect(second))
+            if t == 3:
+                pair_up(a_grouped[:, HALF:SLOTS, 2:4], a_high)
+            nc.vector.tensor_copy(a_grouped[:, 0:HALF, t], wa_planes[t].indirect(first))
+        for c0 in (HALF, 0):
+            quantize(a_op, c0, c0 + HALF, a_grouped[:, c0:c0 + HALF, :])
+
+        x_tiles = [placed("x_tile%d" % c, [P, P, PACK], BF16, (0, 1, 2, 0)[c] * ROW // 2) for c in range(TILES)]
+
+        def interleave_x(c, copy):
+            copy(out=x_tiles[c][:].rearrange("p (c i) t -> p c t i", i=4),
                  in_=x_raw[:, :, c * P:(c + 1) * P].rearrange("p t (c i) -> p c t i", i=4))
+
+        def quantize_x(c):
+            quantize(x_op, c * P, (c + 1) * P, x_tiles[c][:])
+
         for c in range(TILES):
-            quantize(x_op, c * P, (c + 1) * P, x_tiles[c])
+            interleave_x(c, nc.scalar.copy)
+        for c in range(TILES):
+            quantize_x(c)
 
-        squares = keep.tile([P, 3, TILES], F32, name="squares")
-        acc = keep.tile([P, TILES], F32, name="acc")
-        rest = keep.tile([P, TILES], F32, name="rest")
-        partial = keep.tile([P, 2, TILES], F32, name="partial")
+        y_sq, za_sq, ga_sq = [keep.tile([P, TILES], F32, name=name) for name in ("y_sq", "za_sq", "ga_sq")]
+        early_squares = []
 
-        def square(kind, c, src, unused, scale=1.0):
-            nc.scalar.activation(unused[:], src, SQUARE, scale=scale, accum_out=squares[:, kind, c:c + 1])
+        def square(total, src):
+            unused = placed("square%d" % len(early_squares), [P, SLOTS], F32, ROW * (len(early_squares) % 2))
+            early_squares.append(unused)
+            nc.scalar.activation(unused[:], src, SQUARE, accum_out=total)
 
-        def add_half_xx(dst, kind, c, before):
-            nc.scalar.activation(dst[:, c:c + 1], squares[:, kind, c:c + 1], IDENTITY, scale=half_xx[:, c:c + 1],
-                                 bias=before[:, c:c + 1])
-
-        for c in range(3):
-            square(0, c, y_sb[c], scratch_at("y_sq%d" % c, 11776 + 2048 * (c % 2)))
-        za = [scratch("za0"), scratch_at("za1", 16384), scratch("za2")]
+        za = [scratch("za%d" % c) for c in range(3)]
         ga = [scratch("ga%d" % c) for c in range(3)]
+        weights_first = keep.tile([P, LEAD + SLOTS], F32, name="weights0")
+        weights = [weights_first[:, LEAD:LEAD + SLOTS]] + [scratch("weights%d" % c)[:] for c in (1, 2)]
+        for c in range(3):
+            square(y_sq[:, c:c + 1], y_sb[c])
         for c in range(3):
             sa = bank(c)
-            product(sa[:], x_op, c * P, a_op, 0, SLOTS)
-            if c == 0:
-                nc.vector.tensor_tensor(za[c][:], sa[:], ts_all[:], MULT)
-            else:
-                nc.vector.scalar_tensor_tensor(za[c][:], sa[:], us_straight[:, c:c + 1], ts_all[:], MULT, MULT)
+            product(sa[:], c, a_op, 0, SLOTS)
+            nc.vector.scalar_tensor_tensor(za[c][:], sa[:], us_cols[:, c:c + 1], ts_all[:], MULT, MULT)
             if c == 1:
-                nc.vector.scalar_tensor_tensor(ga[0][:], za[0][:], us_straight[:, 0:1], y_sb[0], MULT, SUB)
-        turned_scores = bank(3)
+                for n in range(2):
+                    nc.vector.tensor_tensor(ga[n][:], za[n][:], y_sb[n], SUB)
+        turned = bank(3)
         for b in range(BLOCKS):
-            product(block(turned_scores, b), a_op, b * P, x_op, 3 * P, R)
+            nc.tensor.matmul_mx(
+                out=block(turned, b),
+                lhsT=block(a_op[0], b).bitcast(FP8X4),
+                lhsT_scale=block(a_op[1], b),
+                rhs=block(x_op[0], 3).bitcast(FP8X4),
+                rhs_scale=block(x_op[1], 3),
+                start=True,
+                stop=True,
+            )
         scaled = scratch("scaled")
         for b in range(BLOCKS):
-            nc.scalar.activation(block(scaled, b), block(turned_scores, b), COPY, scale=ts_scale[:, b:b + 1])
+            nc.scalar.activation(block(scaled, b), block(turned, b), COPY, scale=ts_cols[:, b:b + 1])
         ts_sa = bank(4)
         for b in range(BLOCKS):
             nc.tensor.transpose(block(ts_sa, b), block(scaled, b), ident[:])
-        weights = [keep.tile([P, SLOTS + 1], F32, name="weights0")] + [scratch("weights%d" % c) for c in range(1, TILES)]
-        for c in (1, 2):
-            nc.gpsimd.tensor_tensor(ga[c][:], za[c][:], y_sb[c], SUB)
         for c in range(3):
-            nc.gpsimd.tensor_tensor(weights[c][:, 0:SLOTS], ga[c][:], (ts_all if c else ts_first)[:], MULT)
-        closing_weights = weights[0][:, HALF:SLOTS + 1]
-        square(1, 0, za[0][:], scratch("za_sq0"), scale=us_first[:])
-        for c in (1, 2):
-            square(1, c, za[c][:], scratch("za_sq%d" % (c % 2)))
-        square(1, 3, ts_sa[:], scratch("za_sq1"), scale=us_last[:])
-
-        sb = [bank(c) for c in range(3)] + [bank(5)]
-        for c in (2, 3):
-            product(sb[c][:], x_op, c * P, a_op, 0, SLOTS, stop=False)
-        b_op = operand("b", shared.tile([P, SLOTS, PACK], BF16, name="b_grouped", align_bytes=64, offset=16384))
-        gather_operand(b_op, wb_planes, shared.tile([P, 2, SLOTS], F32, name="b_pair", offset=0))
-        ga.append(scratch("wb3"))
-        nc.vector.scalar_tensor_tensor(ga[3][:], ts_sa[:], us_last[:], y_sb[3], MULT, SUB)
-        nc.gpsimd.tensor_tensor(weights[3][:], ga[3][:], ts_all[:], MULT)
-        product(sb[0][:, 0:HALF], x_op, 0, b_op, 0, HALF)
-        product(sb[1][:, 0:HALF], x_op, P, b_op, 0, HALF)
-        product(sb[1][:, HALF:SLOTS], x_op, P, b_op, HALF, SLOTS)
-        for c in (2, 3):
-            product(sb[c][:], x_op, c * P, b_op, 0, SLOTS, start=False)
-        product(closing[:, 0:HALF], x_op, 0, b_op, HALF, SLOTS)
-
-        for c in range(TILES):
-            nc.scalar.activation(partial[:, 0, c:c + 1], squares[:, 1, c:c + 1], COPY, scale=neg_xx[:, c:c + 1])
+            if c == 2:
+                nc.gpsimd.tensor_tensor(ga[c][:], za[c][:], y_sb[c], SUB)
+            nc.gpsimd.tensor_tensor(weights[c], ga[c][:], (ts_all if c else ts_first)[:], MULT)
         for c in range(2):
-            square(2, c, ga[c][:], scratch_at("ga_sq%d" % c, 2048 * c))
-            add_half_xx(partial[:, 1, :], 0, c, partial[:, 0, :])
-            add_half_xx(rest, 2, c, partial[:, 1, :])
-        square(0, 3, y_sb[3], scratch_at("y_sq3", 2048))
-        for c in (2, 3):
-            nc.scalar.activation(rest[:, c:c + 1], squares[:, 0, c:c + 1], IDENTITY, scale=xx_cols[:, c:c + 1],
-                                 bias=partial[:, 0, c:c + 1])
+            square(za_sq[:, c:c + 1], za[c][:])
+        za_late = keep.tile([P, HALF], F32, name="za_late")
+        nc.scalar.activation(za_late[:], ts_sa[:, 0:HALF], COPY, scale=us_last[:])
 
+        b_low = placed("b_low", [P, 2, SLOTS], F32, 4 * ROW - 64)
+        b_grouped = placed("b_grouped", [P, SLOTS, PACK], BF16, 0)
+        nc.vector.tensor_copy(b_low[:, 0, :], wb_planes[0].indirect(offsets[:]))
+        second_plane(b_grouped, b_low, wb_planes[1])
+        rest_scale = placed("rest_scale", [P, TILES], F32, 5 * ROW - 64)
+        nc.scalar.activation(rest_scale[:, 0:2], scale_cols[:, TILES:TILES + 2], COPY, scale=0.5)
+        nc.scalar.copy(out=rest_scale[:, 2:TILES], in_=scale_cols[:, TILES + 2:2 * TILES])
+        sb = [bank(0), bank(1)] + [psum_pair.tile([P, SLOTS], F32, name="summed%d" % n, offset=4 * SLOTS * n)[:]
+                                   for n in range(2)]
+        for c in (2, 3):
+            product(sb[c], c, a_op, 0, SLOTS, stop=False)
+        nc.vector.tensor_copy(b_grouped[:, :, 2], wb_planes[2].indirect(offsets[:]))
+        for c0, half in ((HALF, second), (0, first)):
+            nc.vector.tensor_copy(b_grouped[:, c0:c0 + HALF, 3], wb_planes[3].indirect(half))
+        b_op = operand("b")
+        for c0 in (HALF, 0):
+            quantize(b_op, c0, c0 + HALF, b_grouped[:, c0:c0 + HALF, :])
+        ga_late = [keep.tile([P, HALF], F32, name="ga_late0"), keep.tile([P, HALF], F32, name="wb3")]
+        nc.gpsimd.tensor_tensor(ga_late[0][:], za_late[:], y_sb[3][:, 0:HALF], SUB)
+        nc.vector.scalar_tensor_tensor(ga_late[1][:], ts_sa[:, HALF:SLOTS], us_last[:], y_sb[3][:, HALF:SLOTS], MULT, SUB)
+        weights.append(placed("weights3", [P, SLOTS], F32, 0)[:])
+        for n in range(2):
+            nc.gpsimd.tensor_tensor(weights[3][:, n * HALF:(n + 1) * HALF], ga_late[n][:],
+                                    ts_all[:, n * HALF:(n + 1) * HALF], MULT)
+        product(sb[0][:, HALF:SLOTS], 0, b_op, HALF, SLOTS)
+        product(sb[1][:, HALF:SLOTS], 1, b_op, HALF, SLOTS)
+        product(sb[1][:, 0:HALF], 1, b_op, 0, HALF)
+        for c in (2, 3):
+            product(sb[c], c, b_op, 0, SLOTS, start=False)
+        product(closing[:, LEAD:LEAD + HALF], 0, b_op, 0, HALF)
+
+        rest = keep.tile([P, 2, TILES], F32, name="rest")
+
+        def combine(c):
+            nc.scalar.activation(rest[:, 0, c:c + 1], za_sq[:, c:c + 1], IDENTITY, scale=-1.0, bias=y_sq[:, c:c + 1])
+            if c < 2:
+                nc.scalar.activation(rest[:, 1, c:c + 1], ga_sq[:, c:c + 1], IDENTITY, bias=rest[:, 0, c:c + 1])
+
+        late_squares = ((ga_sq[:, 0:1], ga[0][:], 1.0), (za_sq[:, 2:3], za[2][:], 1.0), (ga_sq[:, 1:2], ga[1][:], 1.0),
+                        (y_sq[:, 3:4], y_sb[3], 1.0), (za_sq[:, 3:4], ts_sa[:], us_last[:]))
+        for n, (total, src, scale) in enumerate(late_squares):
+            unused = placed("late_square%d" % n, [P, SLOTS], BF16, 5 * ROW + (n % 2) * ROW // 2)
+            nc.scalar.activation(unused[:], src, SQUARE, scale=scale, accum_out=total)
         for c in range(TILES):
-            width = HALF if c == 0 else SLOTS
-            nc.vector.scalar_tensor_tensor(scratch("last%d" % c)[:, 0:width], sb[c][:, 0:width], us_xx[:, c:c + 1],
-                                           weights[c][:, 0:width], MULT, MULT, accum_out=acc[:, c:c + 1])
-            total = closing_weights[:, HALF:HALF + 1] if c == 0 else res_cols[:, 32 * c:32 * c + 1]
-            nc.scalar.activation(total, acc[:, c:c + 1], IDENTITY, bias=rest[:, c:c + 1])
-        nc.vector.scalar_tensor_tensor(scratch("last4")[:, 0:HALF + 1], closing[:, 0:HALF + 1], 1.0, closing_weights,
-                                       MULT, MULT, accum_out=res_cols[:, 0:1])
+            combine(c)
+
+        acc = keep.tile([P, TILES], F32, name="acc")
+        for c in range(TILES):
+            c0 = 0 if c else HALF
+            nc.vector.scalar_tensor_tensor(scratch("last%d" % c)[:, c0:SLOTS], sb[c][:, c0:SLOTS],
+                                           us_xx[:, c:c + 1] if c else 1.0,
+                                           weights[c][:, c0:SLOTS], MULT, MULT, accum_out=acc[:, c:c + 1])
+            total = res_cols[:, 32 * c:32 * c + 1] if c else weights_first[:, LEAD - 1:LEAD]
+            nc.scalar.activation(total, rest[:, 1 if c < 2 else 0, c:c + 1], IDENTITY, scale=rest_scale[:, c:c + 1],
+                                 bias=acc[:, c:c + 1])
+        nc.vector.scalar_tensor_tensor(scratch("last4")[:, 0:HALF + 1], closing[:, LEAD - 1:LEAD + HALF], 1.0,
+                                       weights_first[:, LEAD - 1:LEAD + HALF], MULT, MULT, accum_out=res_cols[:, 0:1])
         res_rows = keep.tile([P, P], F32, name="res_rows", align_bytes=64)
         nc.vector.transpose(res_rows[:], res_cols[:])
         nc.sync.dma_start(

@@ -82,7 +82,7 @@ def tile_attend_gtrace_sq_kernel(tc, xT, wa, wb, us, ts, xx, y, offs, out):
 
         ts_win = keep.tile([P, T], F32, name="ts_win")
         row_scales = keep.tile([P, P], F32, name="row_scales")
-        res_cols = keep.tile([P, P], F32, name="res_cols", align_bytes=64)
+        res_cols = keep.tile([P, 32], F32, name="res_cols", align_bytes=64)
         ident = keep.tile([P, P], F32, name="ident")
         ones = keep.tile([P, 1], F32, name="ones")
         nc.vector.memset(row_scales[:], 0.0)
@@ -281,14 +281,14 @@ def tile_attend_gtrace_sq_kernel(tc, xT, wa, wb, us, ts, xx, y, offs, out):
             nc.vector.scalar_tensor_tensor(scratch("last%d" % c)[:, c0:SLOTS], sb[c][:, c0:SLOTS],
                                            us_xx[:, c:c + 1] if c else 1.0,
                                            weights[c][:, c0:SLOTS], MULT, MULT, accum_out=acc[:, c:c + 1])
-            total = res_cols[:, 32 * c:32 * c + 1] if c else weights_first[:, LEAD - 1:LEAD]
+            total = res_cols[:, 8 * c:8 * c + 1] if c else weights_first[:, LEAD - 1:LEAD]
             nc.scalar.activation(total, rest[:, 1 if c < 2 else 0, c:c + 1], IDENTITY, scale=rest_scale[:, c:c + 1],
                                  bias=acc[:, c:c + 1])
         nc.vector.scalar_tensor_tensor(scratch("last4")[:, 0:HALF + 1], closing[:, LEAD - 1:LEAD + HALF], 1.0,
                                        weights_first[:, LEAD - 1:LEAD + HALF], MULT, MULT, accum_out=res_cols[:, 0:1])
-        res_rows = keep.tile([P, P], F32, name="res_rows", align_bytes=64)
+        res_rows = keep.tile([P, 32], F32, name="res_rows", align_bytes=64)
         nc.vector.transpose(res_rows[:], res_cols[:])
         nc.sync.dma_start(
             out=out.rearrange("o (c q j) -> q (o c) j", q=4, j=32),
-            in_=res_rows[0:P:32, :].rearrange("q (c j) -> q c j", j=32),
+            in_=res_rows[0:P:8, :],
         )

@@ -65,12 +65,12 @@ def tile_attend_gtrace_sq_kernel(tc, xT, wa, wb, us, ts, xx, y, offs, out):
         y_v = y.rearrange("(c p) i -> p c i", p=P)
 
         ts_stage = placed("ts_stage", [P, QUARTER], F32, 2752)
-        us_stage = placed("us_stage", [2 * TILES, P], F32, 8 * ROW - 256)
+        us_stage = placed("us_stage", [P, P], F32, 8 * ROW - 256)
         nc.sync.dma_start(out=wa_pairs[0][:], in_=wa_v[:, 0:2, :])
         nc.sync.dma_start(offsets[:], offs)
         nc.scalar.dma_start(out=ts_stage[0:P:32, :], in_=ts[0:1, :].rearrange("o (q w) -> (o q) w", q=4))
-        nc.scalar.dma_start(out=us_stage[0:TILES, :], in_=us.rearrange("(c p) o -> c (p o)", p=P))
-        nc.scalar.dma_start(out=us_stage[TILES:2 * TILES, :], in_=xx.rearrange("(c p) o -> c (p o)", p=P))
+        nc.scalar.dma_start(out=us_stage[64:64 + TILES, :], in_=us.rearrange("(c p) o -> c (p o)", p=P))
+        nc.scalar.dma_start(out=us_stage[64 + TILES:64 + 2 * TILES, :], in_=xx.rearrange("(c p) o -> c (p o)", p=P))
         for t in (2, 3):
             nc.sync.dma_start(out=wa_planes[t], in_=wa_v[:, t, :])
         nc.sync.dma_start(out=x_raw[:], in_=xT.rearrange("(p t) r -> p t r", t=PACK))
@@ -94,10 +94,11 @@ def tile_attend_gtrace_sq_kernel(tc, xT, wa, wb, us, ts, xx, y, offs, out):
         nc.tensor.transpose(closing[:, 0:P], ones[:].to_broadcast([P, P]), ident[:])
         for q in range(4):
             nc.vector.tensor_copy(ts_win[32 * q:32 * q + 1, q * QUARTER:(q + 1) * QUARTER], ts_stage[32 * q:32 * q + 1, :])
-        nc.scalar.activation(row_scales[0:2 * TILES, :], us_stage[:], COPY)
+        nc.scalar.activation(row_scales[64:64 + 2 * TILES, :], us_stage[64:64 + 2 * TILES, :], COPY)
 
-        turned = scale_cols = psum_pair.tile([P, 2 * SLOTS], F32, name="scale_cols", offset=0)
-        nc.tensor.transpose(turned[:, 0:P], row_scales[:], ident[:])
+        scale_banks = psum_pair.tile([P, 2 * SLOTS], F32, name="scale_cols", offset=0)
+        nc.tensor.transpose(scale_banks[:, 0:P], row_scales[:], ident[:])
+        turned = scale_cols = scale_banks[:, 64:P]
         us_cols = placed("us_cols", [P, 32], F32, 5 * ROW - 128)
         nc.scalar.copy(out=us_cols[:, 0:TILES], in_=turned[:, 0:TILES])
         xx_cols = keep.tile([P, TILES], F32, name="xx_cols")

from contextlib import ExitStack

import concourse.mybir as mybir
from concourse.masks import make_identity

D, R, SLOTS, T = 512, 512, 512, 2048
P = 128
PACK = 4
TILES = R // P
BLOCKS = SLOTS // P
HALF = SLOTS // 2
QUARTER = T // 4
LEAD = 16
ROW = 4 * SLOTS

F32 = mybir.dt.float32
BF16 = mybir.dt.bfloat16
U32 = mybir.dt.uint32
U16 = mybir.dt.uint16
U8 = mybir.dt.uint8
FP8X4 = mybir.dt.float8_e4m3fn_x4
ADD = mybir.AluOpType.add
MULT = mybir.AluOpType.mult
SUB = mybir.AluOpType.subtract
AXIS_X = mybir.AxisListType.X
COPY = mybir.ActivationFunctionType.Copy
IDENTITY = mybir.ActivationFunctionType.Identity
SQUARE = mybir.ActivationFunctionType.Square

FLOPS = 2 * 2 * D * R * SLOTS
BYTES = 4 * (D * R + 2 * D * T + 2 * R + T + R * SLOTS + R) + 2 * P * SLOTS // 16


def tile_attend_gtrace_sq_kernel(tc, xT, wa, wb, us, ts, xx, y, offs, out):
    nc = tc.nc
    with ExitStack() as ctx:
        keep = ctx.enter_context(tc.tile_pool(name="keep", bufs=1))
        shared = ctx.enter_context(tc.tile_pool(name="shared", bufs=1))
        psum = ctx.enter_context(tc.psum_pool(name="psum", bufs=1))
        psum_pair = ctx.enter_context(tc.psum_pool(name="psum_pair", bufs=1))

        def bank(n):
            return psum.tile([P, SLOTS], F32, name="bank%d" % n)

        def scratch(name):
            return keep.tile([P, SLOTS], F32, name=name)

        def placed(name, shape, dtype, offset):
            return shared.tile(shape, dtype, name=name, align_bytes=64, offset=offset)

        def block(ap, b):
            return ap[:, b * P:(b + 1) * P]

        offsets = keep.tile([P, SLOTS // 16], U16, name="offsets")
        first, second = offsets[:, 0:HALF // 16], offsets[:, HALF // 16:SLOTS // 16]
        wa_pairs = [keep.tile([P, 2, T], F32, name="wa_pair")]
        wa_planes = [wa_pairs[0][:, t, :] for t in range(2)] + [keep.tile([P, T], F32, name="wa%d" % t)[:] for t in (2, 3)]
        wb_pair = keep.tile([P, 2, T], F32, name="wb_pair")
        wb_planes = [wb_pair[:, t, :] for t in range(2)] + [keep.tile([P, T], F32, name="wb%d" % t)[:] for t in (2, 3)]
        x_raw = keep.tile([P, PACK, R], F32, name="x_raw")
        y_early = keep.tile([P, 3, SLOTS], F32, name="y_early")
        y_sb = [y_early[:, c, :] for c in range(3)] + [scratch("y_late")[:]]
        wa_v = wa.rearrange("(p t) w -> p t w", t=PACK)
        wb_v = wb.rearrange("(p t) w -> p t w", t=PACK)
        y_v = y.rearrange("(c p) i -> p c i", p=P)

        ts_stage = placed("ts_stage", [P, QUARTER], F32, 2752)
        us_stage = placed("us_stage", [P, P], F32, 8 * ROW - 256)
        nc.sync.dma_start(out=wa_pairs[0][:], in_=wa_v[:, 0:2, :])
        nc.sync.dma_start(offsets[:], offs)
        nc.scalar.dma_start(out=ts_stage[0:P:32, :], in_=ts[0:1, :].rearrange("o (q w) -> (o q) w", q=4))
        nc.scalar.dma_start(out=us_stage[64:64 + TILES, :], in_=us.rearrange("(c p) o -> c (p o)", p=P))
        nc.scalar.dma_start(out=us_stage[64 + TILES:64 + 2 * TILES, :], in_=xx.rearrange("(c p) o -> c (p o)", p=P))
        for t in (2, 3):
            nc.sync.dma_start(out=wa_planes[t], in_=wa_v[:, t, :])
        nc.sync.dma_start(out=x_raw[:], in_=xT.rearrange("(p t) r -> p t r", t=PACK))
        nc.sync.dma_start(out=y_early[:], in_=y_v[:, 0:3, :])
        nc.sync.dma_start(out=wb_pair[:], in_=wb_v[:, 0:2, :])
        for t in (2, 3):
            nc.sync.dma_start(out=wb_planes[t], in_=wb_v[:, t, :])
        nc.sync.dma_start(out=y_sb[3], in_=y_v[:, 3, :])

        ts_win = keep.tile([P, T], F32, name="ts_win")
        row_scales = keep.tile([P, P], F32, name="row_scales")
        res_cols = keep.tile([P, 32], F32, name="res_cols", align_bytes=64)
        ident = keep.tile([P, P], F32, name="ident")
        ones = keep.tile([P, 1], F32, name="ones")
        nc.vector.memset(row_scales[:], 0.0)
        nc.vector.memset(ts_win[:], 0.0)
        nc.vector.memset(res_cols[:], 0.0)
        nc.vector.memset(ones[:], 1.0)
        make_identity(nc, ident[:])
        closing = bank(7)
        nc.tensor.transpose(closing[:, 0:P], ones[:].to_broadcast([P, P]), ident[:])
        for q in range(4):
            nc.vector.tensor_copy(ts_win[32 * q:32 * q + 1, q * QUARTER:(q + 1) * QUARTER], ts_stage[32 * q:32 * q + 1, :])
        nc.scalar.activation(row_scales[64:64 + 2 * TILES, :], us_stage[64:64 + 2 * TILES, :], COPY)

        scale_banks = psum_pair.tile([P, 2 * SLOTS], F32, name="scale_cols", offset=0)
        nc.tensor.transpose(scale_banks[:, 0:P], row_scales[:], ident[:])
        turned = scale_cols = scale_banks[:, 64:P]
        us_cols = placed("us_cols", [P, 32], F32, 5 * ROW - 128)
        nc.scalar.copy(out=us_cols[:, 0:TILES], in_=turned[:, 0:TILES])
        xx_cols = keep.tile([P, TILES], F32, name="xx_cols")
        nc.scalar.copy(out=xx_cols[:], in_=turned[:, TILES:2 * TILES])
        us_last = keep.tile([P, 1], F32, name="us_last")
        nc.scalar.copy(out=us_last[:], in_=turned[:, TILES - 1:TILES])
        us_xx = keep.tile([P, TILES], F32, name="us_xx")
        for c in range(TILES):
            nc.scalar.activation(us_xx[:, c:c + 1], turned[:, c:c + 1], COPY, scale=xx_cols[:, c:c + 1])

        def operand(name):
            codes = keep.tile([P, SLOTS], U32, name=name + "_codes", align_bytes=64)
            scales = keep.tile([P, SLOTS], U8, name=name + "_scales", align_bytes=64)
            return codes, scales

        def quantize(op, c0, c1, grouped):
            nc.vector.quantize_mx(
                out=op[0][:, c0:c1].bitcast(FP8X4),
                scales=op[1][:, c0:c1],
                in_=grouped.rearrange("p w t -> p (w t)"),
            )

        def product(dst, c, moving, m0, m1, start=True, stop=True):
            nc.tensor.matmul_mx(
                out=dst,
                lhsT=block(x_op[0], c).bitcast(FP8X4),
                lhsT_scale=block(x_op[1], c),
                rhs=moving[0][:, m0:m1].bitcast(FP8X4),
                rhs_scale=moving[1][:, m0:m1],
                start=start,
                stop=stop,
            )

        def pair_up(grouped, stage):
            nc.scalar.copy(out=grouped, in_=stage.rearrange("p t s -> p s t"))

        def second_plane(grouped, low, plane):
            for c0, half in ((0, first), (HALF, second)):
                nc.vector.tensor_copy(low[:, 1, c0:c0 + HALF], plane.indirect(half))
                pair_up(grouped[:, c0:c0 + HALF, 0:2], low[:, :, c0:c0 + HALF])

        x_op, a_op = operand("x"), operand("a")

        a_grouped = placed("a_grouped", [P, SLOTS, PACK], BF16, 8 * ROW)
        a_low = placed("a_low", [P, 2, SLOTS], F32, 2816)[:]
        a_high = placed("a_high", [P, 2, HALF], F32, 768)[:]
        ts_row = placed("ts_row", [P, SLOTS], F32, 9 * ROW)
        nc.vector.tensor_copy(ts_row[:], ts_win[:].indirect(offsets[:]))
        turned = bank(2)
        for b in range(BLOCKS):
            nc.tensor.transpose(block(turned, b), block(ts_row, b), ident[:])
        nc.vector.tensor_copy(a_low[:, 0, :], wa_planes[0].indirect(offsets[:]))
        ts_cols = keep.tile([P, BLOCKS], F32, name="ts_cols")
        nc.vector.tensor_reduce(ts_cols[:], turned[:].rearrange("p (b q j) -> p b q j", b=BLOCKS, q=4)[:, :, :, 0], AXIS_X, ADD)
        turned = bank(3)
        for b in range(BLOCKS):
            nc.tensor.transpose(block(turned, b), ts_cols[:, b:b + 1].to_broadcast([P, P]), ident[:])
        ts_all = placed("ts_all", [P, SLOTS], F32, 7 * ROW)
        nc.scalar.copy(out=ts_all[:], in_=turned[:])
        ts_first = scratch("ts_first")
        nc.gpsimd.tensor_scalar(ts_first[:], ts_all[:], us_xx[:, 0:1], 0.0, MULT, ADD)
        second_plane(a_grouped, a_low, wa_planes[1])
        for t in (2, 3):
            nc.vector.tensor_copy(a_high[:, t - 2, :], wa_planes[t].indirect(second))
            if t == 3:
                pair_up(a_grouped[:, HALF:SLOTS, 2:4], a_high)
            nc.vector.tensor_copy(a_grouped[:, 0:HALF, t], wa_planes[t].indirect(first))
        for c0 in (HALF, 0):
            quantize(a_op, c0, c0 + HALF, a_grouped[:, c0:c0 + HALF, :])

        x_tiles = [placed("x_tile%d" % c, [P, P, PACK], BF16, (0, 1, 2, 0)[c] * ROW // 2) for c in range(TILES)]

        def interleave_x(c, copy):
            copy(out=x_tiles[c][:].rearrange("p (c i) t -> p c t i", i=4),
                 in_=x_raw[:, :, c * P:(c + 1) * P].rearrange("p t (c i) -> p c t i", i=4))

        def quantize_x(c):
            quantize(x_op, c * P, (c + 1) * P, x_tiles[c][:])

        for c in range(TILES):
            interleave_x(c, nc.scalar.copy)
        for c in range(TILES):
            quantize_x(c)

        y_sq, za_sq, ga_sq = [keep.tile([P, TILES], F32, name=name) for name in ("y_sq", "za_sq", "ga_sq")]
        early_squares = []

        def square(total, src):
            unused = placed("square%d" % len(early_squares), [P, SLOTS], F32, ROW * (len(early_squares) % 2))
            early_squares.append(unused)
            nc.scalar.activation(unused[:], src, SQUARE, accum_out=total)

        za = [scratch("za%d" % c) for c in range(3)]
        ga = [scratch("ga%d" % c) for c in range(3)]
        weights_first = keep.tile([P, LEAD + SLOTS], F32, name="weights0")
        weights = [weights_first[:, LEAD:LEAD + SLOTS]] + [scratch("weights%d" % c)[:] for c in (1, 2)]
        for c in range(3):
            square(y_sq[:, c:c + 1], y_sb[c])
        for c in range(3):
            sa = bank(c)
            product(sa[:], c, a_op, 0, SLOTS)
            nc.vector.scalar_tensor_tensor(za[c][:], sa[:], us_cols[:, c:c + 1], ts_all[:], MULT, MULT)
            if c == 1:
                for n in range(2):
                    nc.vector.tensor_tensor(ga[n][:], za[n][:], y_sb[n], SUB)
        turned = bank(3)
        for b in range(BLOCKS):
            nc.tensor.matmul_mx(
                out=block(turned, b),
                lhsT=block(a_op[0], b).bitcast(FP8X4),
                lhsT_scale=block(a_op[1], b),
                rhs=block(x_op[0], 3).bitcast(FP8X4),
                rhs_scale=block(x_op[1], 3),
                start=True,
                stop=True,
            )
        scaled = scratch("scaled")
        for b in range(BLOCKS):
            nc.scalar.activation(block(scaled, b), block(turned, b), COPY, scale=ts_cols[:, b:b + 1])
        ts_sa = bank(4)
        for b in range(BLOCKS):
            nc.tensor.transpose(block(ts_sa, b), block(scaled, b), ident[:])
        for c in range(3):
            if c == 2:
                nc.gpsimd.tensor_tensor(ga[c][:], za[c][:], y_sb[c], SUB)
            nc.gpsimd.tensor_tensor(weights[c], ga[c][:], (ts_all if c else ts_first)[:], MULT)
        for c in range(2):
            square(za_sq[:, c:c + 1], za[c][:])
        za_late = keep.tile([P, HALF], F32, name="za_late")
        nc.scalar.activation(za_late[:], ts_sa[:, 0:HALF], COPY, scale=us_last[:])

        b_low = placed("b_low", [P, 2, SLOTS], F32, 4 * ROW - 64)
        b_grouped = placed("b_grouped", [P, SLOTS, PACK], BF16, 0)
        nc.vector.tensor_copy(b_low[:, 0, :], wb_planes[0].indirect(offsets[:]))
        second_plane(b_grouped, b_low, wb_planes[1])
        rest_scale = placed("rest_scale", [P, TILES], F32, 5 * ROW - 64)
        nc.scalar.activation(rest_scale[:, 0:2], scale_cols[:, TILES:TILES + 2], COPY, scale=0.5)
        nc.scalar.copy(out=rest_scale[:, 2:TILES], in_=scale_cols[:, TILES + 2:2 * TILES])
        sb = [bank(0), bank(1)] + [psum_pair.tile([P, SLOTS], F32, name="summed%d" % n, offset=4 * SLOTS * n)[:]
                                   for n in range(2)]
        for c in (2, 3):
            product(sb[c], c, a_op, 0, SLOTS, stop=False)
        nc.vector.tensor_copy(b_grouped[:, :, 2], wb_planes[2].indirect(offsets[:]))
        for c0, half in ((HALF, second), (0, first)):
            nc.vector.tensor_copy(b_grouped[:, c0:c0 + HALF, 3], wb_planes[3].indirect(half))
        b_op = operand("b")
        for c0 in (HALF, 0):
            quantize(b_op, c0, c0 + HALF, b_grouped[:, c0:c0 + HALF, :])
        ga_late = [keep.tile([P, HALF], F32, name="ga_late0"), keep.tile([P, HALF], F32, name="wb3")]
        nc.gpsimd.tensor_tensor(ga_late[0][:], za_late[:], y_sb[3][:, 0:HALF], SUB)
        nc.vector.scalar_tensor_tensor(ga_late[1][:], ts_sa[:, HALF:SLOTS], us_last[:], y_sb[3][:, HALF:SLOTS], MULT, SUB)
        weights.append(placed("weights3", [P, SLOTS], F32, 0)[:])
        for n in range(2):
            nc.gpsimd.tensor_tensor(weights[3][:, n * HALF:(n + 1) * HALF], ga_late[n][:],
                                    ts_all[:, n * HALF:(n + 1) * HALF], MULT)
        product(sb[0][:, HALF:SLOTS], 0, b_op, HALF, SLOTS)
        product(sb[1][:, HALF:SLOTS], 1, b_op, HALF, SLOTS)
        product(sb[1][:, 0:HALF], 1, b_op, 0, HALF)
        for c in (2, 3):
            product(sb[c], c, b_op, 0, SLOTS, start=False)
        product(closing[:, LEAD:LEAD + HALF], 0, b_op, 0, HALF)

        rest = keep.tile([P, 2, TILES], F32, name="rest")

        def combine(c):
            nc.scalar.activation(rest[:, 0, c:c + 1], za_sq[:, c:c + 1], IDENTITY, scale=-1.0, bias=y_sq[:, c:c + 1])
            if c < 2:
                nc.scalar.activation(rest[:, 1, c:c + 1], ga_sq[:, c:c + 1], IDENTITY, bias=rest[:, 0, c:c + 1])

        late_squares = ((ga_sq[:, 0:1], ga[0][:], 1.0), (za_sq[:, 2:3], za[2][:], 1.0), (ga_sq[:, 1:2], ga[1][:], 1.0),
                        (y_sq[:, 3:4], y_sb[3], 1.0), (za_sq[:, 3:4], ts_sa[:], us_last[:]))
        for n, (total, src, scale) in enumerate(late_squares):
            unused = placed("late_square%d" % n, [P, SLOTS], BF16, 5 * ROW + (n % 2) * ROW // 2)
            nc.scalar.activation(unused[:], src, SQUARE, scale=scale, accum_out=total)
        for c in range(TILES):
            combine(c)

        acc = keep.tile([P, TILES], F32, name="acc")
        for c in range(TILES):
            c0 = 0 if c else HALF
            nc.vector.scalar_tensor_tensor(scratch("last%d" % c)[:, c0:SLOTS], sb[c][:, c0:SLOTS],
                                           us_xx[:, c:c + 1] if c else 1.0,
                                           weights[c][:, c0:SLOTS], MULT, MULT, accum_out=acc[:, c:c + 1])
            total = res_cols[:, 8 * c:8 * c + 1] if c else weights_first[:, LEAD - 1:LEAD]
            nc.scalar.activation(total, rest[:, 1 if c < 2 else 0, c:c + 1], IDENTITY, scale=rest_scale[:, c:c + 1],
                                 bias=acc[:, c:c + 1])
        nc.vector.scalar_tensor_tensor(scratch("last4")[:, 0:HALF + 1], closing[:, LEAD - 1:LEAD + HALF], 1.0,
                                       weights_first[:, LEAD - 1:LEAD + HALF], MULT, MULT, accum_out=res_cols[:, 0:1])
        res_rows = keep.tile([P, 32], F32, name="res_rows", align_bytes=64)
        nc.vector.transpose(res_rows[:], res_cols[:])
        nc.sync.dma_start(
            out=out.rearrange("o (c q j) -> q (o c) j", q=4, j=32),
            in_=res_rows[0:P:8, :],
        )
